import numpy as np
import ml_dtypes


def mxq(x, axis, fmt="e4m3"):
    dtype, down = {"e4m3": (ml_dtypes.float8_e4m3fn, 7), "e5m2": (ml_dtypes.float8_e5m2, 14)}[fmt]
    v = np.moveaxis(np.asarray(x, np.float32).astype(ml_dtypes.bfloat16).astype(np.float64), axis, -1)
    blocks = v.reshape(v.shape[:-1] + (-1, 32))
    amax = np.abs(blocks).max(-1, keepdims=True)
    byte = np.maximum(np.where(amax > 0, np.frexp(amax)[1] - 1 + 127, 0) - down, 1)
    scale = np.exp2(byte - 127.0)
    codes = (blocks / scale).astype(np.float32).astype(dtype).astype(np.float64)
    return np.moveaxis((codes * scale).reshape(v.shape), -1, axis)


WIDE = False


def mx_kscale(k):
    if not WIDE:
        return np.ones(k)
    levels = np.array([10, -10, 5, -5, 0])
    if k % 512:
        return np.exp2(np.random.permutation(np.resize(levels, k // 32))).repeat(32)
    a = np.empty((k // 512, 16))
    for p in range(k // 512):
        a[p, :8] = np.random.permutation(np.resize(levels, 8))
        for g in range(8):
            far = levels[np.abs(levels - a[p, g]) >= 10]
            a[p, g + 8] = far[np.random.randint(len(far))]
    return np.exp2(a.ravel()).repeat(32)


def f64(x):
    return np.asarray(x).astype(np.float64)


def striped(idx):
    return np.tile(idx.reshape(-1, 16).T, (8, 1)).astype(np.uint16)


def unstriped(offs):
    return offs[:16].T.reshape(-1).astype(np.int64)


E2M1 = np.array([0.0, 0.5, 1.0, 1.5, 2.0, 3.0, 4.0, 6.0, -0.0, -0.5, -1.0, -1.5, -2.0, -3.0, -4.0, -6.0])


def pack_weight(w, fmt):
    k, n = w.shape
    w = f64(np.asarray(w, np.float32).astype(ml_dtypes.bfloat16)).reshape(k // 32, 32, n)
    amax = np.abs(w).max(1)
    if fmt == "e4m3":
        byte = np.frexp(amax)[1] - 1 + 127 - 7
    else:
        mant, ex = np.frexp(amax / 6.0)
        byte = np.where(mant > 0.5, ex, ex - 1) + 127
    byte = np.clip(np.where(amax > 0, byte, 1), 1, 254)
    scaled = (w * np.exp2(127.0 - byte)[:, None, :]).reshape(k, n).astype(np.float32)
    by_word = np.ascontiguousarray(scaled.reshape(k // 512, 128, 4, n).transpose(0, 1, 3, 2))
    if fmt == "e4m3":
        words = by_word.astype(ml_dtypes.float8_e4m3fn).view(np.uint8)
    else:
        c = by_word.astype(ml_dtypes.float4_e2m1fn).view(np.uint8) & 0xF
        words = (c[..., 0::2] | (c[..., 1::2] << 4)).reshape(k // 512, 128, 2 * n)
    return np.ascontiguousarray(words), np.ascontiguousarray(byte.astype(np.uint8).reshape(k // 512, 16, n))


def unpack_weight(words, scales, fmt):
    g, _, n = scales.shape
    words = np.ascontiguousarray(words).reshape(g, 128, n, -1)
    if fmt == "e4m3":
        vals = words.view(ml_dtypes.float8_e4m3fn).astype(np.float64)
    else:
        nib = np.empty((g, 128, n, 4), np.uint8)
        nib[..., 0::2] = words & 0xF
        nib[..., 1::2] = words >> 4
        vals = E2M1[nib]
    vals = vals * np.repeat(np.exp2(scales.astype(np.float64) - 127.0), 8, axis=1)[..., None]
    return vals.transpose(0, 1, 3, 2).reshape(g * 512, n)


def gelu(v):
    return 0.5 * v * (1.0 + np.tanh(np.sqrt(2.0 / np.pi) * (v + 0.044715 * v**3)))


K, T, S, T2, M = 1024, 2048, 512, 2048, 512

def setup_inputs():
    n = np.random.standard_normal
    s = mx_kscale(K)[:, None]
    sm = mx_kscale(M)[:, None]
    tab_words, tab_scales = pack_weight(0.2 * n((K, T)) * s, "e4m3")
    w1_words, w1_scales = pack_weight(3.0 * n((K, K)) / np.sqrt(K) / s, "e2m1")
    w3_words, w3_scales = pack_weight(0.5 * n((M, K)) / np.sqrt(M) / sm / s.T, "e4m3")
    bands = np.random.permutation(T2)
    return {
        "tab_words": tab_words, "tab_scales": tab_scales,
        "offs": striped(np.random.permutation(T)[:S]),
        "xT": (np.round(16 * n((K, T2))) / 16 * s).astype(np.float32),
        "offs2": striped(bands[:S]),
        "offs3": striped(bands[S:2 * S]),
        "w1_words": w1_words, "w1_scales": w1_scales,
        "w2": (0.4 * n((K, K)) / np.sqrt(K) / s).astype(np.float32),
        "w3_words": w3_words, "w3_scales": w3_scales,
        "adj": (n((M, S)) * sm).astype(np.float32),
    }

def reference(tab_words, tab_scales, offs, xT, offs2, offs3, w1_words, w1_scales, w2, w3_words, w3_scales, adj):
    v = unpack_weight(tab_words, tab_scales, "e4m3")[:, unstriped(offs)]
    x = f64(xT)[:, unstriped(offs2)] - f64(xT)[:, unstriped(offs3)]
    w1 = unpack_weight(w1_words, w1_scales, "e2m1")
    w3 = unpack_weight(w3_words, w3_scales, "e4m3")
    a = w1.T @ v + mxq(f64(w2), 0, "e4m3").T @ mxq(x, 0, "e4m3")
    th = np.tanh(a)
    e = w3.T @ mxq(f64(adj), 0, "e4m3")
    h = (1.0 - th * th) * e
    return v.T @ mxq(h, 0, "e4m3")

@@ -1,0 +1,272 @@
+from contextlib import ExitStack
+
+import concourse.mybir as mybir
+from concourse.masks import make_identity
+
+K, T, S, M = 1024, 2048, 512, 512
+FLOPS = 2 * S * (2 * K * K + M * K + K * S)
+
+F32 = mybir.dt.float32
+BF16 = mybir.dt.bfloat16
+I32 = mybir.dt.int32
+U32 = mybir.dt.uint32
+U16 = mybir.dt.uint16
+U8 = mybir.dt.uint8
+FP8X4 = mybir.dt.float8_e4m3fn_x4
+FP4X4 = mybir.dt.float4_e2m1fn_x4
+ACT = mybir.ActivationFunctionType
+ALU = mybir.AluOpType
+
+P = 128
+PACK = 4
+KP = P * PACK
+PASSES = K // KP
+JT = S // P
+QUADS = 4
+
+
+def tile_list_ocean_colour_gradient_kernel(
+    tc, tab_words, tab_scales, offs, xT, offs2, offs3, w1_words, w1_scales, w2, w3_words, w3_scales, adj, out
+):
+    nc = tc.nc
+    with ExitStack() as ctx:
+        keep = ctx.enter_context(tc.tile_pool(name="keep", bufs=1))
+        ring = ctx.enter_context(tc.tile_pool(name="ring", bufs=2))
+        psum = ctx.enter_context(tc.psum_pool(name="psum", bufs=2))
+
+        def held(name, shape, dtype):
+            return keep.tile(shape, dtype, name=name, align_bytes=64)
+
+        idx = keep.tile([P, S // 16], U16, name="idx")
+        idx2 = keep.tile([P, S // 16], U16, name="idx2")
+        idx3 = keep.tile([P, S // 16], U16, name="idx3")
+        planes = [[held("plane%d%d" % (a, t), [P, T], F32) for t in range(PACK)] for a in range(PASSES)]
+        tab_w = [held("tab_w%d" % a, [P, T], U32) for a in range(PASSES)]
+        tab_s = held("tab_s", [P, PASSES, T], U8)
+        w1_w = [held("w1_w%d" % b, [P, PASSES, 2 * KP], U8) for b in range(PASSES)]
+        w1_s = held("w1_s", [P, PASSES, K], U8)
+        w3_w = [held("w3_w%d" % b, [P, KP], U32) for b in range(PASSES)]
+        w3_s = held("w3_s", [P, K], U8)
+        w2_raw = [[held("w2_raw%d%d" % (a, b), [P, PACK, KP], F32) for b in range(PASSES)] for a in range(PASSES)]
+        adj_raw = held("adj_raw", [P, PACK, S], F32)
+        ident = held("ident", [P, P], F32)
+        warm = held("warm", [P, 1], F32)
+
+        nc.vector.memset(tab_s[:].rearrange("p a t -> p (a t)").bitcast(I32), 0)
+        nc.vector.memset(w1_s[:].rearrange("p a t -> p (a t)").bitcast(I32), 0)
+        nc.vector.memset(w3_s[:].bitcast(I32), 0)
+        make_identity(nc, ident[:])
+        nc.scalar.activation(warm[:], ident[:, 0:1], ACT.Tanh)
+
+        x_rows = xT.rearrange("(a p t) c -> a t p c", a=PASSES, t=PACK)
+
+        def load_plane(a, t):
+            nc.sync.dma_start(planes[a][t][:], x_rows[a, t])
+
+        def load_scales(tile, src):
+            for q in range(QUADS):
+                nc.sync.dma_start(
+                    tile[32 * q : 32 * q + 4].bitcast(I32),
+                    src[:, 4 * q : 4 * q + 4, :].rearrange("a r y -> r a y").bitcast(I32),
+                )
+
+        def load_w2(a, b):
+            nc.sync.dma_start(
+                w2_raw[a][b][:],
+                w2[KP * a : KP * (a + 1), KP * b : KP * (b + 1)].rearrange("(p t) c -> p t c", t=PACK),
+            )
+
+        def load_w1(b):
+            nc.sync.dma_start(
+                w1_w[b][:].bitcast(I32),
+                w1_words[:, :, 2 * KP * b : 2 * KP * (b + 1)].rearrange("a p y -> p a y").bitcast(I32),
+            )
+
+        def load_w3(b):
+            nc.sync.dma_start(
+                w3_w[b][:].bitcast(I32),
+                w3_words[0].rearrange("p n t -> p (n t)")[:, PACK * KP * b : PACK * KP * (b + 1)].bitcast(I32),
+            )
+
+        nc.sync.dma_start(idx3[:], offs3)
+        nc.sync.dma_start(idx2[:], offs2)
+        load_plane(0, 0)
+        load_plane(0, 1)
+        nc.sync.dma_start(idx[:], offs)
+        load_plane(0, 2)
+        load_plane(0, 3)
+        load_scales(tab_s, tab_scales)
+        for a in range(PASSES):
+            nc.sync.dma_start(tab_w[a][:].bitcast(I32), tab_words[a].rearrange("p n t -> p (n t)").bitcast(I32))
+        load_plane(1, 0)
+        load_w2(0, 0)
+        load_plane(1, 1)
+        load_w2(1, 0)
+        load_plane(1, 2)
+        load_w2(0, 1)
+        load_scales(w1_s, w1_scales)
+        load_plane(1, 3)
+        load_w1(0)
+        for q in range(QUADS):
+            nc.sync.dma_start(w3_s[32 * q : 32 * q + 4, :].bitcast(I32), w3_scales[0, 4 * q : 4 * q + 4, :].bitcast(I32))
+        nc.sync.dma_start(adj_raw[:], adj.rearrange("(p t) c -> p t c", t=PACK))
+        load_w3(0)
+        load_w2(1, 1)
+        load_w1(1)
+        load_w3(1)
+
+        def weave_views(grouped, raw):
+            return (
+                grouped.rearrange("p (c i t) -> p c t i", i=4, t=PACK),
+                raw.rearrange("p t (c i) -> p c t i", i=4),
+            )
+
+        def quantize(name, grouped, width):
+            codes = held(name + "_c", [P, width], U32)
+            scales = held(name + "_s", [P, width], U8)
+            nc.vector.quantize_mx(out=codes[:].bitcast(FP8X4), scales=scales[:], in_=grouped)
+            return codes, scales
+
+        half = S // 2
+        x_q = {}
+
+        def gather_x(a):
+            diff = ring.tile([P, PACK, S], F32, name="diff")
+            for t in range(PACK):
+                sub = [ring.tile([P, half], F32, name="sub%d" % h) for h in range(2)]
+                for h in range(2):
+                    nc.vector.tensor_copy(sub[h][:], planes[a][t][:].indirect(idx3[:, 16 * h : 16 * (h + 1)]))
+                for h in range(2):
+                    nc.vector.tensor_tensor(
+                        diff[:, t, half * h : half * (h + 1)],
+                        planes[a][t][:].indirect(idx2[:, 16 * h : 16 * (h + 1)]),
+                        sub[h][:],
+                        ALU.subtract,
+                    )
+            for j in range(JT):
+                grouped = ring.tile([P, PACK * P], BF16, name="x_g", align_bytes=64, bufs=4)
+                dst, src = weave_views(grouped[:], diff[:, :, P * j : P * (j + 1)])
+                if a == 0:
+                    nc.scalar.copy(dst, src)
+                else:
+                    nc.vector.tensor_copy(dst, src)
+                x_q[a, j] = quantize("x%d%d" % (a, j), grouped[:], P)
+
+        def weave_quantize(name, raw, engine, negate=False):
+            grouped = ring.tile([P, PACK * KP], BF16, name="wide_g", align_bytes=64)
+            dst, src = weave_views(grouped[:], raw[:])
+            if negate:
+                nc.scalar.activation(dst, src, ACT.Copy, scale=-1.0)
+            elif engine == "scalar":
+                nc.scalar.copy(dst, src)
+            else:
+                nc.vector.tensor_copy(dst, src)
+            return quantize(name, grouped[:], KP)
+
+        gather_x(0)
+        v_w, v_s = [], []
+        for a in range(PASSES):
+            scales = held("v_s%d" % a, [P, S], U8)
+            nc.vector.tensor_copy(scales[:], tab_s[:, a, :].indirect(idx[:]))
+            v_s.append(scales)
+        for a in range(PASSES):
+            words = held("v_w%d" % a, [P, S], U32)
+            nc.vector.tensor_copy(words[:], tab_w[a][:].indirect(idx[:]))
+            v_w.append(words)
+        w2_q = {}
+        w2_q[0, 0] = weave_quantize("w2_00", w2_raw[0][0], "scalar")
+        w2_q[1, 0] = weave_quantize("w2_10", w2_raw[1][0], "scalar")
+        w2_q[0, 1] = weave_quantize("w2_01", w2_raw[0][1], "scalar")
+        gather_x(1)
+        adj_c, adj_s = weave_quantize("adj", adj_raw, "scalar", negate=True)
+        w2_q[1, 1] = weave_quantize("w2_11", w2_raw[1][1], "vector")
+
+        h_q = {}
+        for b in range(PASSES):
+            r = slice(KP * b, KP * (b + 1))
+            for j in range(JT):
+                cols = slice(P * j, P * (j + 1))
+                acc = psum.tile([P, KP], F32, name="acc", tag="acc", bufs=5)
+
+                def x_pass(a):
+                    nc.tensor.matmul_mx(
+                        out=acc[:],
+                        lhsT=x_q[a, j][0][:].bitcast(FP8X4),
+                        lhsT_scale=x_q[a, j][1][:],
+                        rhs=w2_q[a, b][0][:].bitcast(FP8X4),
+                        rhs_scale=w2_q[a, b][1][:],
+                        start=(a == 0),
+                        stop=(a == PASSES - 1),
+                    )
+
+                x_pass(0)
+                for a in range(PASSES):
+                    nc.tensor.matmul_mx(
+                        out=acc[:],
+                        lhsT=v_w[a][:, cols].bitcast(FP8X4),
+                        lhsT_scale=v_s[a][:, cols],
+                        rhs=w1_w[b][:, a, :].bitcast(FP4X4),
+                        rhs_scale=w1_s[:, a, r],
+                        start=False,
+                        stop=False,
+                    )
+                x_pass(1)
+                neg_e = psum.tile([P, KP], F32, name="neg_e", tag="side", bufs=3)
+                nc.tensor.matmul_mx(
+                    out=neg_e[:],
+                    lhsT=adj_c[:, cols].bitcast(FP8X4),
+                    lhsT_scale=adj_s[:, cols],
+                    rhs=w3_w[b][:].bitcast(FP8X4),
+                    rhs_scale=w3_s[:, r],
+                    start=True,
+                    stop=True,
+                )
+                th = ring.tile([P, KP], F32, name="th")
+                nc.scalar.activation(
+                    th[:].rearrange("p (u m e) -> p u m e", u=2, e=2),
+                    acc[:].rearrange("p (m u e) -> p u m e", u=2, e=2),
+                    ACT.Tanh,
+                )
+                th2 = ring.tile([P, KP], F32, name="th2", bufs=4)
+                nc.scalar.activation(th2[:], th[:], ACT.Square)
+                h_rows = ring.tile([P, KP], BF16, name="h_rows", align_bytes=64)
+                for u in range(2):
+                    nc.vector.scalar_tensor_tensor(
+                        h_rows[:, 256 * u : 256 * (u + 1)].rearrange("p (m e) -> p m e", e=2),
+                        th2[:, 256 * u : 256 * (u + 1)].rearrange("p (m e) -> p m e", e=2),
+                        1.0,
+                        neg_e[:].rearrange("p (m u e) -> p u m e", u=2, e=2)[:, u],
+                        ALU.subtract,
+                        ALU.mult,
+                    )
+                turned = psum.tile([P, 2, P], F32, name="turned", tag="side", bufs=3)
+                for u in range(2):
+                    nc.tensor.transpose(turned[:, u, :], h_rows[:].bitcast(F32)[:, P * u : P * (u + 1)], ident[:])
+                grouped = ring.tile([P, PACK * P], BF16, name="h_g", align_bytes=64)
+                nc.vector.tensor_copy(
+                    grouped[:].bitcast(F32).rearrange("p (j u) -> p j u", u=2),
+                    turned[:].rearrange("p u j -> p j u"),
+                )
+                h_q[b, j] = quantize("h%d%d" % (b, j), grouped[:], P)
+
+        out_rows = out.rearrange("(n p) j -> p n j", p=P)
+        for j in range(JT):
+            res = psum.tile([P, JT, P], F32, name="res", tag="acc", bufs=5)
+            for n in range(JT):
+                cols = slice(P * n, P * (n + 1))
+                for b in range(PASSES):
+                    nc.tensor.matmul_mx(
+                        out=res[:, n, :],
+                        lhsT=v_w[b][:, cols].bitcast(FP8X4),
+                        lhsT_scale=v_s[b][:, cols],
+                        rhs=h_q[b, j][0][:].bitcast(FP8X4),
+                        rhs_scale=h_q[b, j][1][:],
+                        start=(b == 0),
+                        stop=(b == PASSES - 1),
+                    )
+            staged = ring.tile([P, JT, P], F32, name="staged", bufs=4)
+            if j % 2 == 0:
+                nc.vector.tensor_copy(staged[:], res[:])
+            else:
+                nc.scalar.copy(staged[:], res[:])
+            nc.sync.dma_start(out_rows[:, :, P * j : P * (j + 1)], staged[:])

@@ -37,12 +37,16 @@ def tile_list_ocean_colour_gradient_kernel(
         def held(name, shape, dtype):
             return keep.tile(shape, dtype, name=name, align_bytes=64)
 
+        def bank(name, shape, tag):
+            return psum.tile(shape, F32, name=name, tag=tag, bufs={"A": 5, "B": 0, "C": 3}[tag])
+
         idx = keep.tile([P, S // 16], U16, name="idx")
         idx2 = keep.tile([P, S // 16], U16, name="idx2")
         idx3 = keep.tile([P, S // 16], U16, name="idx3")
         planes = [[held("plane%d%d" % (a, t), [P, T], F32) for t in range(PACK)] for a in range(PASSES)]
         tab_w = [held("tab_w%d" % a, [P, T], U32) for a in range(PASSES)]
-        tab_s = held("tab_s", [P, PASSES, T], U8)
+        tab_s = held("tab_s", [P, T], U8)
+        v_s = [held("v_s%d" % a, [P, S], U8) for a in range(PASSES)]
         w1_w = [held("w1_w%d" % b, [P, PASSES, 2 * KP], U8) for b in range(PASSES)]
         w1_s = held("w1_s", [P, PASSES, K], U8)
         w3_w = [held("w3_w%d" % b, [P, KP], U32) for b in range(PASSES)]
@@ -52,23 +56,30 @@ def tile_list_ocean_colour_gradient_kernel(
         ident = held("ident", [P, P], F32)
         warm = held("warm", [P, 1], F32)
 
-        nc.vector.memset(tab_s[:].rearrange("p a t -> p (a t)").bitcast(I32), 0)
+        nc.vector.memset(tab_s[:].bitcast(I32), 0)
         nc.vector.memset(w1_s[:].rearrange("p a t -> p (a t)").bitcast(I32), 0)
         nc.vector.memset(w3_s[:].bitcast(I32), 0)
+        nc.vector.memset(v_s[1][:].bitcast(I32), 0)
         make_identity(nc, ident[:])
         nc.scalar.activation(warm[:], ident[:, 0:1], ACT.Tanh)
+
+        for q in range(QUADS):
+            nc.gpsimd.dma_start(tab_s[32 * q : 32 * q + 8, :].bitcast(I32), tab_scales[:, 4 * q : 4 * q + 4, :].bitcast(I32))
+        for q in range(QUADS):
+            nc.gpsimd.dma_start(
+                w1_s[32 * q : 32 * q + 4].bitcast(I32),
+                w1_scales[:, 4 * q : 4 * q + 4, :].rearrange("a r y -> r a y").bitcast(I32),
+            )
+        for q in range(QUADS):
+            nc.gpsimd.dma_start(w3_s[32 * q : 32 * q + 4, :].bitcast(I32), w3_scales[0, 4 * q : 4 * q + 4, :].bitcast(I32))
 
         x_rows = xT.rearrange("(a p t) c -> a t p c", a=PASSES, t=PACK)
 
         def load_plane(a, t):
             nc.sync.dma_start(planes[a][t][:], x_rows[a, t])
 
-        def load_scales(tile, src):
-            for q in range(QUADS):
-                nc.sync.dma_start(
-                    tile[32 * q : 32 * q + 4].bitcast(I32),
-                    src[:, 4 * q : 4 * q + 4, :].rearrange("a r y -> r a y").bitcast(I32),
-                )
+        def load_table(a):
+            nc.sync.dma_start(tab_w[a][:].bitcast(I32), tab_words[a].rearrange("p n t -> p (n t)").bitcast(I32))
 
         def load_w2(a, b):
             nc.sync.dma_start(
@@ -88,38 +99,33 @@ def tile_list_ocean_colour_gradient_kernel(
                 w3_words[0].rearrange("p n t -> p (n t)")[:, PACK * KP * b : PACK * KP * (b + 1)].bitcast(I32),
             )
 
+        def load_adj():
+            nc.sync.dma_start(adj_raw[:], adj.rearrange("(p t) c -> p t c", t=PACK))
+
         nc.sync.dma_start(idx3[:], offs3)
         nc.sync.dma_start(idx2[:], offs2)
         load_plane(0, 0)
-        load_plane(0, 1)
         nc.sync.dma_start(idx[:], offs)
+        nc.vector.tensor_copy(v_s[0][:], tab_s[:].indirect(idx[:]))
+        nc.scalar.dma_start(v_s[1][0:100, :].bitcast(I32), v_s[0][4:104, :].bitcast(I32))
+        load_plane(0, 1)
         load_plane(0, 2)
         load_plane(0, 3)
-        load_scales(tab_s, tab_scales)
-        for a in range(PASSES):
-            nc.sync.dma_start(tab_w[a][:].bitcast(I32), tab_words[a].rearrange("p n t -> p (n t)").bitcast(I32))
+        load_table(0)
+        load_table(1)
         load_plane(1, 0)
         load_w2(0, 0)
         load_plane(1, 1)
         load_w2(1, 0)
         load_plane(1, 2)
-        load_w2(0, 1)
-        load_scales(w1_s, w1_scales)
+        load_adj()
         load_plane(1, 3)
         load_w1(0)
-        for q in range(QUADS):
-            nc.sync.dma_start(w3_s[32 * q : 32 * q + 4, :].bitcast(I32), w3_scales[0, 4 * q : 4 * q + 4, :].bitcast(I32))
-        nc.sync.dma_start(adj_raw[:], adj.rearrange("(p t) c -> p t c", t=PACK))
         load_w3(0)
-        load_w2(1, 1)
         load_w1(1)
+        load_w2(0, 1)
+        load_w2(1, 1)
         load_w3(1)
-
-        def weave_views(grouped, raw):
-            return (
-                grouped.rearrange("p (c i t) -> p c t i", i=4, t=PACK),
-                raw.rearrange("p t (c i) -> p c t i", i=4),
-            )
 
         def quantize(name, grouped, width):
             codes = held(name + "_c", [P, width], U32)
@@ -127,10 +133,21 @@ def tile_list_ocean_colour_gradient_kernel(
             nc.vector.quantize_mx(out=codes[:].bitcast(FP8X4), scales=scales[:], in_=grouped)
             return codes, scales
 
-        half = S // 2
+        def turn_and_quantize(name, rows, on_scalar, tag):
+            turned = bank("turned", [P, 2, P], tag)
+            for u in range(2):
+                nc.tensor.transpose(turned[:, u, :], rows[u].bitcast(F32), ident[:])
+            grouped = ring.tile([P, PACK * P], BF16, name="grouped", align_bytes=64, bufs=3)
+            (nc.scalar.copy if on_scalar else nc.vector.tensor_copy)(
+                grouped[:].bitcast(F32).rearrange("p (j u) -> p j u", u=2),
+                turned[:].rearrange("p u j -> p j u"),
+            )
+            return quantize(name, grouped[:], P)
+
         x_q = {}
 
-        def gather_x(a):
+        def make_x(a):
+            half = S // 2
             diff = ring.tile([P, PACK, S], F32, name="diff")
             for t in range(PACK):
                 sub = [ring.tile([P, half], F32, name="sub%d" % h) for h in range(2)]
@@ -145,48 +162,49 @@ def tile_list_ocean_colour_gradient_kernel(
                     )
             for j in range(JT):
                 grouped = ring.tile([P, PACK * P], BF16, name="x_g", align_bytes=64, bufs=4)
-                dst, src = weave_views(grouped[:], diff[:, :, P * j : P * (j + 1)])
-                if a == 0:
+                dst = grouped[:].rearrange("p (c i t) -> p c t i", i=4, t=PACK)
+                src = diff[:, :, P * j : P * (j + 1)].rearrange("p t (c i) -> p c t i", i=4)
+                if a == 0 or j in (0, 1, 2, 3):
                     nc.scalar.copy(dst, src)
                 else:
                     nc.vector.tensor_copy(dst, src)
                 x_q[a, j] = quantize("x%d%d" % (a, j), grouped[:], P)
 
-        def weave_quantize(name, raw, engine, negate=False):
+        def weave_quantize(name, raw, engine):
             grouped = ring.tile([P, PACK * KP], BF16, name="wide_g", align_bytes=64)
-            dst, src = weave_views(grouped[:], raw[:])
-            if negate:
+            dst = grouped[:].rearrange("p (c i t) -> p c t i", i=4, t=PACK)
+            src = raw[:].rearrange("p t (c i) -> p c t i", i=4)
+            if engine == "S-":
                 nc.scalar.activation(dst, src, ACT.Copy, scale=-1.0)
-            elif engine == "scalar":
+            elif engine == "V-":
+                nc.vector.tensor_scalar(dst, src, -1.0, None, ALU.mult)
+            elif engine == "S":
                 nc.scalar.copy(dst, src)
             else:
                 nc.vector.tensor_copy(dst, src)
             return quantize(name, grouped[:], KP)
 
-        gather_x(0)
-        v_w, v_s = [], []
-        for a in range(PASSES):
-            scales = held("v_s%d" % a, [P, S], U8)
-            nc.vector.tensor_copy(scales[:], tab_s[:, a, :].indirect(idx[:]))
-            v_s.append(scales)
+        make_x(0)
+        v_w = []
         for a in range(PASSES):
             words = held("v_w%d" % a, [P, S], U32)
             nc.vector.tensor_copy(words[:], tab_w[a][:].indirect(idx[:]))
             v_w.append(words)
         w2_q = {}
-        w2_q[0, 0] = weave_quantize("w2_00", w2_raw[0][0], "scalar")
-        w2_q[1, 0] = weave_quantize("w2_10", w2_raw[1][0], "scalar")
-        w2_q[0, 1] = weave_quantize("w2_01", w2_raw[0][1], "scalar")
-        gather_x(1)
-        adj_c, adj_s = weave_quantize("adj", adj_raw, "scalar", negate=True)
-        w2_q[1, 1] = weave_quantize("w2_11", w2_raw[1][1], "vector")
+        w2_q[0, 0] = weave_quantize("w2_00", w2_raw[0][0], "S")
+        w2_q[1, 0] = weave_quantize("w2_10", w2_raw[1][0], "S")
+        adj_c, adj_s = weave_quantize("adj", adj_raw, "S-")
+        make_x(1)
+        w2_q[0, 1] = weave_quantize("w2_01", w2_raw[0][1], "V")
+        w2_q[1, 1] = weave_quantize("w2_11", w2_raw[1][1], "V")
 
         h_q = {}
         for b in range(PASSES):
             r = slice(KP * b, KP * (b + 1))
             for j in range(JT):
+                unit = JT * b + j
                 cols = slice(P * j, P * (j + 1))
-                acc = psum.tile([P, KP], F32, name="acc", tag="acc", bufs=5)
+                acc = bank("acc", [P, KP], "AAAAAAAA"[unit])
 
                 def x_pass(a):
                     nc.tensor.matmul_mx(
@@ -195,11 +213,12 @@ def tile_list_ocean_colour_gradient_kernel(
                         lhsT_scale=x_q[a, j][1][:],
                         rhs=w2_q[a, b][0][:].bitcast(FP8X4),
                         rhs_scale=w2_q[a, b][1][:],
-                        start=(a == 0),
+                        start=(a == 0 and b == 0),
                         stop=(a == PASSES - 1),
                     )
 
-                x_pass(0)
+                if b == 0:
+                    x_pass(0)
                 for a in range(PASSES):
                     nc.tensor.matmul_mx(
                         out=acc[:],
@@ -207,11 +226,13 @@ def tile_list_ocean_colour_gradient_kernel(
                         lhsT_scale=v_s[a][:, cols],
                         rhs=w1_w[b][:, a, :].bitcast(FP4X4),
                         rhs_scale=w1_s[:, a, r],
-                        start=False,
+                        start=(a == 0 and b == 1),
                         stop=False,
                     )
+                if b == 1:
+                    x_pass(0)
                 x_pass(1)
-                neg_e = psum.tile([P, KP], F32, name="neg_e", tag="side", bufs=3)
+                neg_e = bank("neg_e", [P, KP], "CCCCCCCC"[unit])
                 nc.tensor.matmul_mx(
                     out=neg_e[:],
                     lhsT=adj_c[:, cols].bitcast(FP8X4),
@@ -221,15 +242,18 @@ def tile_list_ocean_colour_gradient_kernel(
                     start=True,
                     stop=True,
                 )
-                th = ring.tile([P, KP], F32, name="th")
+                th = ring.tile([P, KP], F32, name="th", bufs=3)
                 nc.scalar.activation(
                     th[:].rearrange("p (u m e) -> p u m e", u=2, e=2),
                     acc[:].rearrange("p (m u e) -> p u m e", u=2, e=2),
                     ACT.Tanh,
                 )
                 th2 = ring.tile([P, KP], F32, name="th2", bufs=4)
-                nc.scalar.activation(th2[:], th[:], ACT.Square)
-                h_rows = ring.tile([P, KP], BF16, name="h_rows", align_bytes=64)
+                if unit in ():
+                    nc.vector.tensor_tensor(th2[:], th[:], th[:], ALU.mult)
+                else:
+                    nc.scalar.activation(th2[:], th[:], ACT.Square)
+                h_rows = ring.tile([P, KP], BF16, name="h_rows", align_bytes=64, bufs=3)
                 for u in range(2):
                     nc.vector.scalar_tensor_tensor(
                         h_rows[:, 256 * u : 256 * (u + 1)].rearrange("p (m e) -> p m e", e=2),
@@ -239,19 +263,13 @@ def tile_list_ocean_colour_gradient_kernel(
                         ALU.subtract,
                         ALU.mult,
                     )
-                turned = psum.tile([P, 2, P], F32, name="turned", tag="side", bufs=3)
-                for u in range(2):
-                    nc.tensor.transpose(turned[:, u, :], h_rows[:].bitcast(F32)[:, P * u : P * (u + 1)], ident[:])
-                grouped = ring.tile([P, PACK * P], BF16, name="h_g", align_bytes=64)
-                nc.vector.tensor_copy(
-                    grouped[:].bitcast(F32).rearrange("p (j u) -> p j u", u=2),
-                    turned[:].rearrange("p u j -> p j u"),
+                h_q[b, j] = turn_and_quantize(
+                    "h%d%d" % (b, j), [h_rows[:, 0:256], h_rows[:, 256:512]], unit in (4,5,6,7), "CCCCCCCC"[unit]
                 )
-                h_q[b, j] = quantize("h%d%d" % (b, j), grouped[:], P)
 
         out_rows = out.rearrange("(n p) j -> p n j", p=P)
         for j in range(JT):
-            res = psum.tile([P, JT, P], F32, name="res", tag="acc", bufs=5)
+            res = bank("res", [P, JT, P], "AAAA"[j])
             for n in range(JT):
                 cols = slice(P * n, P * (n + 1))
                 for b in range(PASSES):
@@ -265,7 +283,7 @@ def tile_list_ocean_colour_gradient_kernel(
                         stop=(b == PASSES - 1),
                     )
             staged = ring.tile([P, JT, P], F32, name="staged", bufs=4)
-            if j % 2 == 0:
+            if j in (0, 2):
                 nc.vector.tensor_copy(staged[:], res[:])
             else:
                 nc.scalar.copy(staged[:], res[:])

@@ -22,6 +22,7 @@ PACK = 4
 KP = P * PACK
 PASSES = K // KP
 JT = S // P
+HALF = S // 2
 QUADS = 4
 
 
@@ -32,13 +33,13 @@ def tile_list_ocean_colour_gradient_kernel(
     with ExitStack() as ctx:
         keep = ctx.enter_context(tc.tile_pool(name="keep", bufs=1))
         ring = ctx.enter_context(tc.tile_pool(name="ring", bufs=2))
-        psum = ctx.enter_context(tc.psum_pool(name="psum", bufs=2))
+        psum = ctx.enter_context(tc.psum_pool(name="psum", bufs=1))
 
-        def held(name, shape, dtype):
-            return keep.tile(shape, dtype, name=name, align_bytes=64)
+        def held(name, shape, dtype, place_of=None):
+            return keep.tile(shape, dtype, name=name, tag=place_of or name, align_bytes=64)
 
-        def bank(name, shape, tag):
-            return psum.tile(shape, F32, name=name, tag=tag, bufs={"A": 5, "B": 0, "C": 3}[tag])
+        def bank(name, shape, number):
+            return psum.tile(shape, F32, name=name, tag="bank%d" % number)
 
         idx = keep.tile([P, S // 16], U16, name="idx")
         idx2 = keep.tile([P, S // 16], U16, name="idx2")
@@ -47,12 +48,12 @@ def tile_list_ocean_colour_gradient_kernel(
         tab_w = [held("tab_w%d" % a, [P, T], U32) for a in range(PASSES)]
         tab_s = held("tab_s", [P, T], U8)
         v_s = [held("v_s%d" % a, [P, S], U8) for a in range(PASSES)]
-        w1_w = [held("w1_w%d" % b, [P, PASSES, 2 * KP], U8) for b in range(PASSES)]
+        w1_w = held("w1_w", [P, PASSES, 2 * K], U8)
         w1_s = held("w1_s", [P, PASSES, K], U8)
         w3_w = [held("w3_w%d" % b, [P, KP], U32) for b in range(PASSES)]
         w3_s = held("w3_s", [P, K], U8)
         w2_raw = [[held("w2_raw%d%d" % (a, b), [P, PACK, KP], F32) for b in range(PASSES)] for a in range(PASSES)]
-        adj_raw = held("adj_raw", [P, PACK, S], F32)
+        adj_raw = [held("adj_raw%d" % h, [P, PACK, HALF], F32) for h in range(2)]
         ident = held("ident", [P, P], F32)
         warm = held("warm", [P, 1], F32)
 
@@ -64,7 +65,9 @@ def tile_list_ocean_colour_gradient_kernel(
         nc.scalar.activation(warm[:], ident[:, 0:1], ACT.Tanh)
 
         for q in range(QUADS):
-            nc.gpsimd.dma_start(tab_s[32 * q : 32 * q + 8, :].bitcast(I32), tab_scales[:, 4 * q : 4 * q + 4, :].bitcast(I32))
+            for a in range(PASSES):
+                row = 32 * q + 4 * a
+                nc.gpsimd.dma_start(tab_s[row : row + 4, :].bitcast(I32), tab_scales[a, 4 * q : 4 * q + 4, :].bitcast(I32))
         for q in range(QUADS):
             nc.gpsimd.dma_start(
                 w1_s[32 * q : 32 * q + 4].bitcast(I32),
@@ -87,44 +90,34 @@ def tile_list_ocean_colour_gradient_kernel(
                 w2[KP * a : KP * (a + 1), KP * b : KP * (b + 1)].rearrange("(p t) c -> p t c", t=PACK),
             )
 
-        def load_w1(b):
-            nc.sync.dma_start(
-                w1_w[b][:].bitcast(I32),
-                w1_words[:, :, 2 * KP * b : 2 * KP * (b + 1)].rearrange("a p y -> p a y").bitcast(I32),
-            )
-
         def load_w3(b):
             nc.sync.dma_start(
                 w3_w[b][:].bitcast(I32),
                 w3_words[0].rearrange("p n t -> p (n t)")[:, PACK * KP * b : PACK * KP * (b + 1)].bitcast(I32),
             )
 
-        def load_adj():
-            nc.sync.dma_start(adj_raw[:], adj.rearrange("(p t) c -> p t c", t=PACK))
-
+        load_plane(0, 0)
         nc.sync.dma_start(idx3[:], offs3)
         nc.sync.dma_start(idx2[:], offs2)
-        load_plane(0, 0)
+        for t in range(1, PACK):
+            load_plane(0, t)
+        load_plane(1, 0)
         nc.sync.dma_start(idx[:], offs)
         nc.vector.tensor_copy(v_s[0][:], tab_s[:].indirect(idx[:]))
         nc.scalar.dma_start(v_s[1][0:100, :].bitcast(I32), v_s[0][4:104, :].bitcast(I32))
-        load_plane(0, 1)
-        load_plane(0, 2)
-        load_plane(0, 3)
         load_table(0)
-        load_table(1)
-        load_plane(1, 0)
-        load_w2(0, 0)
         load_plane(1, 1)
-        load_w2(1, 0)
+        load_table(1)
+        load_w2(0, 0)
         load_plane(1, 2)
-        load_adj()
+        load_w2(1, 0)
+        nc.sync.dma_start(w1_w[:].bitcast(I32), w1_words.rearrange("a p y -> p a y").bitcast(I32))
         load_plane(1, 3)
-        load_w1(0)
-        load_w3(0)
-        load_w1(1)
         load_w2(0, 1)
         load_w2(1, 1)
+        load_w3(0)
+        for h in range(2):
+            nc.sync.dma_start(adj_raw[h][:], adj.rearrange("(p t) c -> p t c", t=PACK)[:, :, HALF * h : HALF * (h + 1)])
         load_w3(1)
 
         def quantize(name, grouped, width):
@@ -133,158 +126,173 @@ def tile_list_ocean_colour_gradient_kernel(
             nc.vector.quantize_mx(out=codes[:].bitcast(FP8X4), scales=scales[:], in_=grouped)
             return codes, scales
 
-        def turn_and_quantize(name, rows, on_scalar, tag):
-            turned = bank("turned", [P, 2, P], tag)
-            for u in range(2):
-                nc.tensor.transpose(turned[:, u, :], rows[u].bitcast(F32), ident[:])
-            grouped = ring.tile([P, PACK * P], BF16, name="grouped", align_bytes=64, bufs=3)
-            (nc.scalar.copy if on_scalar else nc.vector.tensor_copy)(
-                grouped[:].bitcast(F32).rearrange("p (j u) -> p j u", u=2),
-                turned[:].rearrange("p u j -> p j u"),
+        def group_views(grouped, raw):
+            return (
+                grouped.rearrange("p (c i t) -> p c t i", i=4, t=PACK),
+                raw.rearrange("p t (c i) -> p c t i", i=4),
             )
-            return quantize(name, grouped[:], P)
 
-        x_q = {}
+        def round_and_quantize(name, raw, round_copy):
+            width = raw.shape[2]
+            grouped = ring.tile([P, PACK * width], BF16, name="wide_g", align_bytes=64)
+            round_copy(*group_views(grouped[:], raw[:]))
+            return quantize(name, grouped[:], width)
 
-        def make_x(a):
-            half = S // 2
-            diff = ring.tile([P, PACK, S], F32, name="diff")
-            for t in range(PACK):
-                sub = [ring.tile([P, half], F32, name="sub%d" % h) for h in range(2)]
+        def negate_on_vector(dst, src):
+            nc.vector.tensor_scalar(dst, src, -1.0, None, ALU.mult)
+
+        def x_first_pass():
+            turned = []
+            for u in range(2):
+                sums = [bank("x_sum", [P, 2, 2, P], 4 + 2 * u + h) for h in range(2)]
+                for e in range(2):
+                    plane = planes[0][2 * u + e]
+                    plus = ring.tile([P, S], F32, name="plus")
+                    minus = ring.tile([P, S], F32, name="minus")
+                    picked = ring.tile([P, S], F32, name="picked")
+                    nc.vector.tensor_copy(picked[:], plane[:].indirect(idx3[:]))
+                    nc.scalar.activation(minus[:], picked[:], ACT.Copy, scale=-1.0)
+                    nc.vector.tensor_copy(plus[:], plane[:].indirect(idx2[:]))
+                    for j in range(JT):
+                        cols = slice(P * j, P * (j + 1))
+                        dst = sums[j // 2][:, j % 2, e, :]
+                        nc.tensor.matmul(dst, minus[:, cols], ident[:], start=True, stop=False, is_transpose=True)
+                        nc.tensor.matmul(dst, plus[:, cols], ident[:], start=False, stop=True, is_transpose=True)
                 for h in range(2):
-                    nc.vector.tensor_copy(sub[h][:], planes[a][t][:].indirect(idx3[:, 16 * h : 16 * (h + 1)]))
+                    pairs = ring.tile([P, 2, 2 * P], BF16, name="x_pairs", align_bytes=64)
+                    nc.scalar.copy(
+                        pairs[:].rearrange("p j (m e) -> p j m e", e=2),
+                        sums[h][:].rearrange("p j e m -> p j m e"),
+                    )
+                    if u == 0:
+                        turned.append(bank("x_turned", [P, 2, 2, P], 4 + h))
+                    for j in range(2):
+                        nc.tensor.transpose(turned[h][:, j, u, :], pairs[:, j, :].bitcast(F32), ident[:])
+            codes = held("x0_c", [P, S], U32, place_of="plane10")
+            scales = held("x0_s", [P, S], U8)
+            for h in range(2):
+                grouped = ring.tile([P, PACK * HALF], BF16, name="x0_g", align_bytes=64)
+                nc.scalar.copy(
+                    grouped[:].bitcast(F32).rearrange("p (j m u) -> p j m u", j=2, u=2),
+                    turned[h][:].rearrange("p j u m -> p j m u"),
+                )
+                cols = slice(HALF * h, HALF * (h + 1))
+                nc.vector.quantize_mx(out=codes[:, cols].bitcast(FP8X4), scales=scales[:, cols], in_=grouped[:])
+            return codes, scales
+
+        def x_second_pass():
+            diff = held("diff", [P, PACK, S], F32)
+            for t in range(PACK):
+                subtrahend = [ring.tile([P, HALF], F32, name="subtrahend%d" % h) for h in range(2)]
+                for h in range(2):
+                    nc.vector.tensor_copy(subtrahend[h][:], planes[1][t][:].indirect(idx3[:, 16 * h : 16 * (h + 1)]))
                 for h in range(2):
                     nc.vector.tensor_tensor(
-                        diff[:, t, half * h : half * (h + 1)],
-                        planes[a][t][:].indirect(idx2[:, 16 * h : 16 * (h + 1)]),
-                        sub[h][:],
+                        diff[:, t, HALF * h : HALF * (h + 1)],
+                        planes[1][t][:].indirect(idx2[:, 16 * h : 16 * (h + 1)]),
+                        subtrahend[h][:],
                         ALU.subtract,
                     )
+            codes = held("x1_c", [P, S], U32)
+            scales = held("x1_s", [P, S], U8)
             for j in range(JT):
-                grouped = ring.tile([P, PACK * P], BF16, name="x_g", align_bytes=64, bufs=4)
-                dst = grouped[:].rearrange("p (c i t) -> p c t i", i=4, t=PACK)
-                src = diff[:, :, P * j : P * (j + 1)].rearrange("p t (c i) -> p c t i", i=4)
-                if a == 0 or j in (0, 1, 2, 3):
-                    nc.scalar.copy(dst, src)
-                else:
-                    nc.vector.tensor_copy(dst, src)
-                x_q[a, j] = quantize("x%d%d" % (a, j), grouped[:], P)
+                cols = slice(P * j, P * (j + 1))
+                grouped = ring.tile([P, PACK * P], BF16, name="x1_g", align_bytes=64, bufs=JT)
+                nc.vector.tensor_copy(*group_views(grouped[:], diff[:, :, cols]))
+                nc.vector.quantize_mx(out=codes[:, cols].bitcast(FP8X4), scales=scales[:, cols], in_=grouped[:])
+            return codes, scales
 
-        def weave_quantize(name, raw, engine):
-            grouped = ring.tile([P, PACK * KP], BF16, name="wide_g", align_bytes=64)
-            dst = grouped[:].rearrange("p (c i t) -> p c t i", i=4, t=PACK)
-            src = raw[:].rearrange("p t (c i) -> p c t i", i=4)
-            if engine == "S-":
-                nc.scalar.activation(dst, src, ACT.Copy, scale=-1.0)
-            elif engine == "V-":
-                nc.vector.tensor_scalar(dst, src, -1.0, None, ALU.mult)
-            elif engine == "S":
-                nc.scalar.copy(dst, src)
-            else:
-                nc.vector.tensor_copy(dst, src)
-            return quantize(name, grouped[:], KP)
-
-        make_x(0)
+        x_q = [x_first_pass()]
         v_w = []
         for a in range(PASSES):
             words = held("v_w%d" % a, [P, S], U32)
             nc.vector.tensor_copy(words[:], tab_w[a][:].indirect(idx[:]))
             v_w.append(words)
         w2_q = {}
-        w2_q[0, 0] = weave_quantize("w2_00", w2_raw[0][0], "S")
-        w2_q[1, 0] = weave_quantize("w2_10", w2_raw[1][0], "S")
-        adj_c, adj_s = weave_quantize("adj", adj_raw, "S-")
-        make_x(1)
-        w2_q[0, 1] = weave_quantize("w2_01", w2_raw[0][1], "V")
-        w2_q[1, 1] = weave_quantize("w2_11", w2_raw[1][1], "V")
+        for a, b in ((0, 0), (1, 0), (0, 1)):
+            w2_q[a, b] = round_and_quantize("w2_%d%d" % (a, b), w2_raw[a][b], nc.scalar.copy)
+        x_q.append(x_second_pass())
+        w2_q[1, 1] = round_and_quantize("w2_11", w2_raw[1][1], nc.vector.tensor_copy)
+        neg_adj_q = [round_and_quantize("adj%d" % h, adj_raw[h], negate_on_vector) for h in range(2)]
 
         h_q = {}
-        for b in range(PASSES):
-            r = slice(KP * b, KP * (b + 1))
-            for j in range(JT):
-                unit = JT * b + j
-                cols = slice(P * j, P * (j + 1))
-                acc = bank("acc", [P, KP], "AAAAAAAA"[unit])
-
-                def x_pass(a):
-                    nc.tensor.matmul_mx(
-                        out=acc[:],
-                        lhsT=x_q[a, j][0][:].bitcast(FP8X4),
-                        lhsT_scale=x_q[a, j][1][:],
-                        rhs=w2_q[a, b][0][:].bitcast(FP8X4),
-                        rhs_scale=w2_q[a, b][1][:],
-                        start=(a == 0 and b == 0),
-                        stop=(a == PASSES - 1),
-                    )
-
-                if b == 0:
-                    x_pass(0)
-                for a in range(PASSES):
-                    nc.tensor.matmul_mx(
-                        out=acc[:],
-                        lhsT=v_w[a][:, cols].bitcast(FP8X4),
-                        lhsT_scale=v_s[a][:, cols],
-                        rhs=w1_w[b][:, a, :].bitcast(FP4X4),
-                        rhs_scale=w1_s[:, a, r],
-                        start=(a == 0 and b == 1),
-                        stop=False,
-                    )
-                if b == 1:
-                    x_pass(0)
-                x_pass(1)
-                neg_e = bank("neg_e", [P, KP], "CCCCCCCC"[unit])
-                nc.tensor.matmul_mx(
-                    out=neg_e[:],
-                    lhsT=adj_c[:, cols].bitcast(FP8X4),
-                    lhsT_scale=adj_s[:, cols],
-                    rhs=w3_w[b][:].bitcast(FP8X4),
-                    rhs_scale=w3_s[:, r],
-                    start=True,
-                    stop=True,
-                )
-                th = ring.tile([P, KP], F32, name="th", bufs=3)
-                nc.scalar.activation(
-                    th[:].rearrange("p (u m e) -> p u m e", u=2, e=2),
-                    acc[:].rearrange("p (m u e) -> p u m e", u=2, e=2),
-                    ACT.Tanh,
-                )
-                th2 = ring.tile([P, KP], F32, name="th2", bufs=4)
-                if unit in ():
-                    nc.vector.tensor_tensor(th2[:], th[:], th[:], ALU.mult)
-                else:
-                    nc.scalar.activation(th2[:], th[:], ACT.Square)
-                h_rows = ring.tile([P, KP], BF16, name="h_rows", align_bytes=64, bufs=3)
-                for u in range(2):
-                    nc.vector.scalar_tensor_tensor(
-                        h_rows[:, 256 * u : 256 * (u + 1)].rearrange("p (m e) -> p m e", e=2),
-                        th2[:, 256 * u : 256 * (u + 1)].rearrange("p (m e) -> p m e", e=2),
-                        1.0,
-                        neg_e[:].rearrange("p (m u e) -> p u m e", u=2, e=2)[:, u],
-                        ALU.subtract,
-                        ALU.mult,
-                    )
-                h_q[b, j] = turn_and_quantize(
-                    "h%d%d" % (b, j), [h_rows[:, 0:256], h_rows[:, 256:512]], unit in (4,5,6,7), "CCCCCCCC"[unit]
-                )
-
+        tanh_a = held("tanh_a", [P, JT, KP], F32, place_of="w2_raw01")
         out_rows = out.rearrange("(n p) j -> p n j", p=P)
-        for j in range(JT):
-            res = bank("res", [P, JT, P], "AAAA"[j])
-            for n in range(JT):
-                cols = slice(P * n, P * (n + 1))
-                for b in range(PASSES):
+
+        def h_tile(b, j):
+            number = JT * b + j
+            r = slice(KP * b, KP * (b + 1))
+            cols = slice(P * j, P * (j + 1))
+            acc = bank("acc", [P, KP], number)
+            for a in range(PASSES):
+                nc.tensor.matmul_mx(
+                    out=acc[:],
+                    lhsT=v_w[a][:, cols].bitcast(FP8X4),
+                    lhsT_scale=v_s[a][:, cols],
+                    rhs=w1_w[:, a, 2 * KP * b : 2 * KP * (b + 1)].bitcast(FP4X4),
+                    rhs_scale=w1_s[:, a, r],
+                    start=(a == 0),
+                    stop=False,
+                )
+            for a in range(PASSES):
+                nc.tensor.matmul_mx(
+                    out=acc[:],
+                    lhsT=x_q[a][0][:, cols].bitcast(FP8X4),
+                    lhsT_scale=x_q[a][1][:, cols],
+                    rhs=w2_q[a, b][0][:].bitcast(FP8X4),
+                    rhs_scale=w2_q[a, b][1][:],
+                    start=False,
+                    stop=(a == PASSES - 1),
+                )
+            th = tanh_a[:, j, :]
+            nc.scalar.activation(th, acc[:], ACT.Tanh)
+            th2 = ring.tile([P, KP], F32, name="th2", bufs=JT)
+            nc.scalar.activation(th2[:], th, ACT.Square)
+            neg_e = bank("neg_e", [P, KP], number)
+            adj_cols = slice(P * (j % 2), P * (j % 2 + 1))
+            nc.tensor.matmul_mx(
+                out=neg_e[:],
+                lhsT=neg_adj_q[j // 2][0][:, adj_cols].bitcast(FP8X4),
+                lhsT_scale=neg_adj_q[j // 2][1][:, adj_cols],
+                rhs=w3_w[b][:].bitcast(FP8X4),
+                rhs_scale=w3_s[:, r],
+                start=True,
+                stop=True,
+            )
+            h_rows = ring.tile([P, KP], BF16, name="h_rows", align_bytes=64, bufs=3)
+            nc.vector.scalar_tensor_tensor(h_rows[:], th2[:], 1.0, neg_e[:], ALU.subtract, ALU.mult)
+            turned = bank("h_turned", [P, 2, P], number)
+            for u in range(2):
+                nc.tensor.transpose(turned[:, u, :], h_rows[:].bitcast(F32)[:, u::2], ident[:])
+            grouped = ring.tile([P, PACK * P], BF16, name="h_g", align_bytes=64, bufs=3)
+            copy_out = nc.vector.tensor_copy if b == 0 else nc.scalar.copy
+            copy_out(
+                grouped[:].bitcast(F32).rearrange("p (j u) -> p j u", u=2),
+                turned[:].rearrange("p u j -> p j u"),
+            )
+            h_q[b, j] = quantize("h%d%d" % (b, j), grouped[:], P)
+
+        def out_tile(j):
+            res = bank("res", [P, JT, P], j)
+            for b in range(PASSES):
+                for n in range(JT):
+                    cols = slice(P * n, P * (n + 1))
                     nc.tensor.matmul_mx(
                         out=res[:, n, :],
                         lhsT=v_w[b][:, cols].bitcast(FP8X4),
                         lhsT_scale=v_s[b][:, cols],
                         rhs=h_q[b, j][0][:].bitcast(FP8X4),
                         rhs_scale=h_q[b, j][1][:],
-                        start=(b == 0),
-                        stop=(b == PASSES - 1),
+                        start=(b == 0 and n == 0),
+                        stop=(b == PASSES - 1 and n == JT - 1),
                     )
-            staged = ring.tile([P, JT, P], F32, name="staged", bufs=4)
-            if j in (0, 2):
-                nc.vector.tensor_copy(staged[:], res[:])
-            else:
-                nc.scalar.copy(staged[:], res[:])
+            staged = ring.tile([P, JT, P], F32, name="staged", bufs=JT)
+            copy_out = nc.scalar.copy if j % 2 == 0 else nc.vector.tensor_copy
+            copy_out(staged[:], res[:])
             nc.sync.dma_start(out_rows[:, :, P * j : P * (j + 1)], staged[:])
+
+        for b in range(PASSES):
+            for j in range(JT):
+                h_tile(b, j)
+        for j in range(JT):
+            out_tile(j)

@@ -50,7 +50,7 @@ def tile_list_ocean_colour_gradient_kernel(
         v_s = [held("v_s%d" % a, [P, S], U8) for a in range(PASSES)]
         w1_w = held("w1_w", [P, PASSES, 2 * K], U8)
         w1_s = held("w1_s", [P, PASSES, K], U8)
-        w3_w = [held("w3_w%d" % b, [P, KP], U32) for b in range(PASSES)]
+        w3_w = held("w3_w", [P, K], U32)
         w3_s = held("w3_s", [P, K], U8)
         w2_raw = [[held("w2_raw%d%d" % (a, b), [P, PACK, KP], F32) for b in range(PASSES)] for a in range(PASSES)]
         adj_raw = [held("adj_raw%d" % h, [P, PACK, HALF], F32) for h in range(2)]
@@ -63,18 +63,6 @@ def tile_list_ocean_colour_gradient_kernel(
         nc.vector.memset(v_s[1][:].bitcast(I32), 0)
         make_identity(nc, ident[:])
         nc.scalar.activation(warm[:], ident[:, 0:1], ACT.Tanh)
-
-        for q in range(QUADS):
-            for a in range(PASSES):
-                row = 32 * q + 4 * a
-                nc.gpsimd.dma_start(tab_s[row : row + 4, :].bitcast(I32), tab_scales[a, 4 * q : 4 * q + 4, :].bitcast(I32))
-        for q in range(QUADS):
-            nc.gpsimd.dma_start(
-                w1_s[32 * q : 32 * q + 4].bitcast(I32),
-                w1_scales[:, 4 * q : 4 * q + 4, :].rearrange("a r y -> r a y").bitcast(I32),
-            )
-        for q in range(QUADS):
-            nc.gpsimd.dma_start(w3_s[32 * q : 32 * q + 4, :].bitcast(I32), w3_scales[0, 4 * q : 4 * q + 4, :].bitcast(I32))
 
         x_rows = xT.rearrange("(a p t) c -> a t p c", a=PASSES, t=PACK)
 
@@ -90,18 +78,23 @@ def tile_list_ocean_colour_gradient_kernel(
                 w2[KP * a : KP * (a + 1), KP * b : KP * (b + 1)].rearrange("(p t) c -> p t c", t=PACK),
             )
 
-        def load_w3(b):
-            nc.sync.dma_start(
-                w3_w[b][:].bitcast(I32),
-                w3_words[0].rearrange("p n t -> p (n t)")[:, PACK * KP * b : PACK * KP * (b + 1)].bitcast(I32),
-            )
-
         load_plane(0, 0)
         nc.sync.dma_start(idx3[:], offs3)
         nc.sync.dma_start(idx2[:], offs2)
-        for t in range(1, PACK):
-            load_plane(0, t)
+        load_plane(0, 1)
+        for a in range(PASSES):
+            for q in range(QUADS):
+                row = 32 * q + 4 * a
+                nc.sync.dma_start(tab_s[row : row + 4, :].bitcast(I32), tab_scales[a, 4 * q : 4 * q + 4, :].bitcast(I32))
+            load_plane(0, 2 + a)
+        for q in range(QUADS):
+            nc.sync.dma_start(
+                w1_s[32 * q : 32 * q + 4].bitcast(I32),
+                w1_scales[:, 4 * q : 4 * q + 4, :].rearrange("a r y -> r a y").bitcast(I32),
+            )
         load_plane(1, 0)
+        for q in range(QUADS):
+            nc.sync.dma_start(w3_s[32 * q : 32 * q + 4, :].bitcast(I32), w3_scales[0, 4 * q : 4 * q + 4, :].bitcast(I32))
         nc.sync.dma_start(idx[:], offs)
         nc.vector.tensor_copy(v_s[0][:], tab_s[:].indirect(idx[:]))
         nc.scalar.dma_start(v_s[1][0:100, :].bitcast(I32), v_s[0][4:104, :].bitcast(I32))
@@ -115,10 +108,9 @@ def tile_list_ocean_colour_gradient_kernel(
         load_plane(1, 3)
         load_w2(0, 1)
         load_w2(1, 1)
-        load_w3(0)
+        nc.sync.dma_start(w3_w[:].bitcast(I32), w3_words[0].rearrange("p n t -> p (n t)").bitcast(I32))
         for h in range(2):
             nc.sync.dma_start(adj_raw[h][:], adj.rearrange("(p t) c -> p t c", t=PACK)[:, :, HALF * h : HALF * (h + 1)])
-        load_w3(1)
 
         def quantize(name, grouped, width):
             codes = held(name + "_c", [P, width], U32)
@@ -244,7 +236,7 @@ def tile_list_ocean_colour_gradient_kernel(
                     start=False,
                     stop=(a == PASSES - 1),
                 )
-            th = tanh_a[:, j, :]
+            th = tanh_a[:, 2 * b + j % 2, :]
             nc.scalar.activation(th, acc[:], ACT.Tanh)
             th2 = ring.tile([P, KP], F32, name="th2", bufs=JT)
             nc.scalar.activation(th2[:], th, ACT.Square)
@@ -254,7 +246,7 @@ def tile_list_ocean_colour_gradient_kernel(
                 out=neg_e[:],
                 lhsT=neg_adj_q[j // 2][0][:, adj_cols].bitcast(FP8X4),
                 lhsT_scale=neg_adj_q[j // 2][1][:, adj_cols],
-                rhs=w3_w[b][:].bitcast(FP8X4),
+                rhs=w3_w[:, r].bitcast(FP8X4),
                 rhs_scale=w3_s[:, r],
                 start=True,
                 stop=True,
@@ -265,7 +257,7 @@ def tile_list_ocean_colour_gradient_kernel(
             for u in range(2):
                 nc.tensor.transpose(turned[:, u, :], h_rows[:].bitcast(F32)[:, u::2], ident[:])
             grouped = ring.tile([P, PACK * P], BF16, name="h_g", align_bytes=64, bufs=3)
-            copy_out = nc.vector.tensor_copy if b == 0 else nc.scalar.copy
+            copy_out = nc.vector.tensor_copy if j < 2 else nc.scalar.copy
             copy_out(
                 grouped[:].bitcast(F32).rearrange("p (j u) -> p j u", u=2),
                 turned[:].rearrange("p u j -> p j u"),
@@ -287,12 +279,13 @@ def tile_list_ocean_colour_gradient_kernel(
                         stop=(b == PASSES - 1 and n == JT - 1),
                     )
             staged = ring.tile([P, JT, P], F32, name="staged", bufs=JT)
-            copy_out = nc.scalar.copy if j % 2 == 0 else nc.vector.tensor_copy
+            copy_out = nc.vector.tensor_copy if j < 2 else nc.scalar.copy
             copy_out(staged[:], res[:])
             nc.sync.dma_start(out_rows[:, :, P * j : P * (j + 1)], staged[:])
 
-        for b in range(PASSES):
-            for j in range(JT):
-                h_tile(b, j)
+        for h in range(2):
+            for b in range(PASSES):
+                for j in (2 * h, 2 * h + 1):
+                    h_tile(b, j)
         for j in range(JT):
             out_tile(j)

@@ -48,9 +48,9 @@ def tile_list_ocean_colour_gradient_kernel(
         tab_w = [held("tab_w%d" % a, [P, T], U32) for a in range(PASSES)]
         tab_s = held("tab_s", [P, T], U8)
         v_s = [held("v_s%d" % a, [P, S], U8) for a in range(PASSES)]
-        w1_w = held("w1_w", [P, PASSES, 2 * K], U8)
+        w1_w = [held("w1_w%d" % b, [P, PASSES, 2 * KP], U8) for b in range(PASSES)]
         w1_s = held("w1_s", [P, PASSES, K], U8)
-        w3_w = held("w3_w", [P, K], U32)
+        w3_w = [held("w3_w%d" % b, [P, KP], U32) for b in range(PASSES)]
         w3_s = held("w3_s", [P, K], U8)
         w2_raw = [[held("w2_raw%d%d" % (a, b), [P, PACK, KP], F32) for b in range(PASSES)] for a in range(PASSES)]
         adj_raw = [held("adj_raw%d" % h, [P, PACK, HALF], F32) for h in range(2)]
@@ -78,6 +78,19 @@ def tile_list_ocean_colour_gradient_kernel(
                 w2[KP * a : KP * (a + 1), KP * b : KP * (b + 1)].rearrange("(p t) c -> p t c", t=PACK),
             )
 
+        def load_w1(b):
+            nc.sync.dma_start(
+                w1_w[b][:].bitcast(I32),
+                w1_words[:, :, 2 * KP * b : 2 * KP * (b + 1)].rearrange("a p y -> p a y").bitcast(I32),
+            )
+
+        def load_adj(h):
+            nc.sync.dma_start(adj_raw[h][:], adj.rearrange("(p t) c -> p t c", t=PACK)[:, :, HALF * h : HALF * (h + 1)])
+
+        def load_w3(b):
+            words = w3_words[0].rearrange("p n t -> p (n t)").bitcast(I32)
+            nc.sync.dma_start(w3_w[b][:].bitcast(I32), words[:, KP * b : KP * (b + 1)])
+
         load_plane(0, 0)
         nc.sync.dma_start(idx3[:], offs3)
         nc.sync.dma_start(idx2[:], offs2)
@@ -98,25 +111,21 @@ def tile_list_ocean_colour_gradient_kernel(
         nc.sync.dma_start(idx[:], offs)
         nc.vector.tensor_copy(v_s[0][:], tab_s[:].indirect(idx[:]))
         nc.scalar.dma_start(v_s[1][0:100, :].bitcast(I32), v_s[0][4:104, :].bitcast(I32))
-        load_table(0)
         load_plane(1, 1)
-        load_table(1)
-        load_w2(0, 0)
         load_plane(1, 2)
-        load_w2(1, 0)
-        nc.sync.dma_start(w1_w[:].bitcast(I32), w1_words.rearrange("a p y -> p a y").bitcast(I32))
+        load_w2(0, 0)
         load_plane(1, 3)
+        load_w2(1, 0)
+        load_w1(0)
+        load_table(0)
+        load_table(1)
         load_w2(0, 1)
+        load_w1(1)
         load_w2(1, 1)
-        nc.sync.dma_start(w3_w[:].bitcast(I32), w3_words[0].rearrange("p n t -> p (n t)").bitcast(I32))
-        for h in range(2):
-            nc.sync.dma_start(adj_raw[h][:], adj.rearrange("(p t) c -> p t c", t=PACK)[:, :, HALF * h : HALF * (h + 1)])
-
-        def quantize(name, grouped, width):
-            codes = held(name + "_c", [P, width], U32)
-            scales = held(name + "_s", [P, width], U8)
-            nc.vector.quantize_mx(out=codes[:].bitcast(FP8X4), scales=scales[:], in_=grouped)
-            return codes, scales
+        load_adj(0)
+        load_w3(0)
+        load_adj(1)
+        load_w3(1)
 
         def group_views(grouped, raw):
             return (
@@ -124,21 +133,33 @@ def tile_list_ocean_colour_gradient_kernel(
                 raw.rearrange("p t (c i) -> p c t i", i=4),
             )
 
-        def round_and_quantize(name, raw, round_copy):
-            width = raw.shape[2]
-            grouped = ring.tile([P, PACK * width], BF16, name="wide_g", align_bytes=64)
-            round_copy(*group_views(grouped[:], raw[:]))
-            return quantize(name, grouped[:], width)
+        def round_and_quantize(name, parts, round_copies, codes_place=None):
+            width = parts[0].shape[2]
+            codes = held(name + "_c", [P, width * len(parts)], U32, place_of=codes_place)
+            scales = held(name + "_s", [P, width * len(parts)], U8)
+            grouped = []
+            for i, raw in enumerate(parts):
+                tile = held("%s_g%d" % (name, i), [P, PACK * width], BF16)
+                round_copies[i](*group_views(tile[:], raw))
+                grouped.append(tile)
+            for i, tile in enumerate(grouped):
+                cols = slice(width * i, width * (i + 1))
+                nc.vector.quantize_mx(out=codes[:, cols].bitcast(FP8X4), scales=scales[:, cols], in_=tile[:])
+            return codes, scales
+
+        def halves(raw):
+            width = raw.shape[2] // 2
+            return [raw[:, :, width * h : width * (h + 1)] for h in range(2)]
 
         def negate_on_vector(dst, src):
             nc.vector.tensor_scalar(dst, src, -1.0, None, ALU.mult)
 
-        def x_first_pass():
+        def x_pass(a, codes_place):
             turned = []
             for u in range(2):
                 sums = [bank("x_sum", [P, 2, 2, P], 4 + 2 * u + h) for h in range(2)]
                 for e in range(2):
-                    plane = planes[0][2 * u + e]
+                    plane = planes[a][2 * u + e]
                     plus = ring.tile([P, S], F32, name="plus")
                     minus = ring.tile([P, S], F32, name="minus")
                     picked = ring.tile([P, S], F32, name="picked")
@@ -160,10 +181,10 @@ def tile_list_ocean_colour_gradient_kernel(
                         turned.append(bank("x_turned", [P, 2, 2, P], 4 + h))
                     for j in range(2):
                         nc.tensor.transpose(turned[h][:, j, u, :], pairs[:, j, :].bitcast(F32), ident[:])
-            codes = held("x0_c", [P, S], U32, place_of="plane10")
-            scales = held("x0_s", [P, S], U8)
+            codes = held("x%d_c" % a, [P, S], U32, place_of=codes_place)
+            scales = held("x%d_s" % a, [P, S], U8)
             for h in range(2):
-                grouped = ring.tile([P, PACK * HALF], BF16, name="x0_g", align_bytes=64)
+                grouped = ring.tile([P, PACK * HALF], BF16, name="x_g", align_bytes=64)
                 nc.scalar.copy(
                     grouped[:].bitcast(F32).rearrange("p (j m u) -> p j m u", j=2, u=2),
                     turned[h][:].rearrange("p j u m -> p j m u"),
@@ -172,99 +193,108 @@ def tile_list_ocean_colour_gradient_kernel(
                 nc.vector.quantize_mx(out=codes[:, cols].bitcast(FP8X4), scales=scales[:, cols], in_=grouped[:])
             return codes, scales
 
-        def x_second_pass():
-            diff = held("diff", [P, PACK, S], F32)
-            for t in range(PACK):
-                subtrahend = [ring.tile([P, HALF], F32, name="subtrahend%d" % h) for h in range(2)]
-                for h in range(2):
-                    nc.vector.tensor_copy(subtrahend[h][:], planes[1][t][:].indirect(idx3[:, 16 * h : 16 * (h + 1)]))
-                for h in range(2):
-                    nc.vector.tensor_tensor(
-                        diff[:, t, HALF * h : HALF * (h + 1)],
-                        planes[1][t][:].indirect(idx2[:, 16 * h : 16 * (h + 1)]),
-                        subtrahend[h][:],
-                        ALU.subtract,
-                    )
-            codes = held("x1_c", [P, S], U32)
-            scales = held("x1_s", [P, S], U8)
-            for j in range(JT):
-                cols = slice(P * j, P * (j + 1))
-                grouped = ring.tile([P, PACK * P], BF16, name="x1_g", align_bytes=64, bufs=JT)
-                nc.vector.tensor_copy(*group_views(grouped[:], diff[:, :, cols]))
-                nc.vector.quantize_mx(out=codes[:, cols].bitcast(FP8X4), scales=scales[:, cols], in_=grouped[:])
-            return codes, scales
+        on_scalar, on_vector = nc.scalar.copy, nc.vector.tensor_copy
 
-        x_q = [x_first_pass()]
-        v_w = []
-        for a in range(PASSES):
+        def gather_table(a):
             words = held("v_w%d" % a, [P, S], U32)
-            nc.vector.tensor_copy(words[:], tab_w[a][:].indirect(idx[:]))
-            v_w.append(words)
-        w2_q = {}
-        for a, b in ((0, 0), (1, 0), (0, 1)):
-            w2_q[a, b] = round_and_quantize("w2_%d%d" % (a, b), w2_raw[a][b], nc.scalar.copy)
-        x_q.append(x_second_pass())
-        w2_q[1, 1] = round_and_quantize("w2_11", w2_raw[1][1], nc.vector.tensor_copy)
-        neg_adj_q = [round_and_quantize("adj%d" % h, adj_raw[h], negate_on_vector) for h in range(2)]
+            for h in range(2):
+                nc.vector.tensor_copy(words[:, HALF * h : HALF * (h + 1)], tab_w[a][:].indirect(idx[:, 16 * h : 16 * (h + 1)]))
+            return words
+
+        def prepare_w2(a, b, round_copies, codes_place=None):
+            return round_and_quantize("w2_%d%d" % (a, b), halves(w2_raw[a][b][:]), round_copies, codes_place)
+
+        def prepare_adj(h):
+            return round_and_quantize("adj%d" % h, halves(adj_raw[h][:]), [negate_on_vector] * 2)
+
+        x_q = [x_pass(0, "plane11")]
+        w2_q = {(0, 0): prepare_w2(0, 0, [on_scalar] * 2, "plane13")}
+        w2_q[1, 0] = prepare_w2(1, 0, [on_vector] * 2)
+        v_w = [gather_table(0)]
+        x_q.append(x_pass(1, "tab_w0"))
+        v_w.append(gather_table(1))
+        w2_q[0, 1] = prepare_w2(0, 1, [on_vector] * 2)
+        w2_q[1, 1] = prepare_w2(1, 1, [on_vector] * 2)
+        neg_adj_q = [prepare_adj(h) for h in range(2)]
+
+        def square_on_scalar(dst, src):
+            nc.scalar.activation(dst, src, ACT.Square)
+
+        def square_on_vector(dst, src):
+            nc.vector.tensor_tensor(dst, src, src, ALU.mult)
+
+        def square_on_gpsimd(dst, src):
+            nc.gpsimd.tensor_tensor(dst, src, src, ALU.mult)
 
         h_q = {}
-        tanh_a = held("tanh_a", [P, JT, KP], F32, place_of="w2_raw01")
+        th = {}
+        th2 = {}
+        h_rows = {}
+        th2_place = [["plane00", "plane01", "plane02", "plane03"], ["plane10", "plane12", "w2_raw10", "w2_raw00"]]
         out_rows = out.rearrange("(n p) j -> p n j", p=P)
 
-        def h_tile(b, j):
-            number = JT * b + j
+        def a_tile(b, j):
             r = slice(KP * b, KP * (b + 1))
             cols = slice(P * j, P * (j + 1))
-            acc = bank("acc", [P, KP], number)
-            for a in range(PASSES):
+            acc = bank("acc", [P, KP], JT * b + j)
+            table = [
+                (v_w[a][:, cols], v_s[a][:, cols], w1_w[b][:, a, :].bitcast(FP4X4), w1_s[:, a, r]) for a in range(PASSES)
+            ]
+            bands = [
+                (x_q[a][0][:, cols], x_q[a][1][:, cols], w2_q[a, b][0][:].bitcast(FP8X4), w2_q[a, b][1][:])
+                for a in range(PASSES)
+            ]
+            passes = [bands[0], table[0], bands[1], table[1]] if b == 0 else table + bands
+            for i, (words, scale, rhs, rhs_scale) in enumerate(passes):
                 nc.tensor.matmul_mx(
                     out=acc[:],
-                    lhsT=v_w[a][:, cols].bitcast(FP8X4),
-                    lhsT_scale=v_s[a][:, cols],
-                    rhs=w1_w[:, a, 2 * KP * b : 2 * KP * (b + 1)].bitcast(FP4X4),
-                    rhs_scale=w1_s[:, a, r],
-                    start=(a == 0),
-                    stop=False,
+                    lhsT=words.bitcast(FP8X4),
+                    lhsT_scale=scale,
+                    rhs=rhs,
+                    rhs_scale=rhs_scale,
+                    start=(i == 0),
+                    stop=(i == len(passes) - 1),
                 )
-            for a in range(PASSES):
-                nc.tensor.matmul_mx(
-                    out=acc[:],
-                    lhsT=x_q[a][0][:, cols].bitcast(FP8X4),
-                    lhsT_scale=x_q[a][1][:, cols],
-                    rhs=w2_q[a, b][0][:].bitcast(FP8X4),
-                    rhs_scale=w2_q[a, b][1][:],
-                    start=False,
-                    stop=(a == PASSES - 1),
-                )
-            th = tanh_a[:, 2 * b + j % 2, :]
-            nc.scalar.activation(th, acc[:], ACT.Tanh)
-            th2 = ring.tile([P, KP], F32, name="th2", bufs=JT)
-            nc.scalar.activation(th2[:], th, ACT.Square)
+            th[b, j] = ring.tile([P, KP], F32, name="th", bufs=JT)
+            nc.scalar.activation(th[b, j][:], acc[:], ACT.Tanh)
+
+        def square_tile(b, j, square):
+            th2[b, j] = held("th2_%d%d" % (b, j), [P, KP], F32, place_of=th2_place[b][j])
+            square(th2[b, j][:], th[b, j][:])
+
+        def h_product(b, j):
+            number = JT * b + j
+            r = slice(KP * b, KP * (b + 1))
             neg_e = bank("neg_e", [P, KP], number)
             adj_cols = slice(P * (j % 2), P * (j % 2 + 1))
             nc.tensor.matmul_mx(
                 out=neg_e[:],
                 lhsT=neg_adj_q[j // 2][0][:, adj_cols].bitcast(FP8X4),
                 lhsT_scale=neg_adj_q[j // 2][1][:, adj_cols],
-                rhs=w3_w[:, r].bitcast(FP8X4),
+                rhs=w3_w[b][:].bitcast(FP8X4),
                 rhs_scale=w3_s[:, r],
                 start=True,
                 stop=True,
             )
-            h_rows = ring.tile([P, KP], BF16, name="h_rows", align_bytes=64, bufs=3)
-            nc.vector.scalar_tensor_tensor(h_rows[:], th2[:], 1.0, neg_e[:], ALU.subtract, ALU.mult)
+            h_rows[b, j] = held("h_rows%d%d" % (b, j), [P, KP], BF16)
+            nc.vector.scalar_tensor_tensor(h_rows[b, j][:], th2[b, j][:], 1.0, neg_e[:], ALU.subtract, ALU.mult)
+
+        def h_turn(b, j, copy_out):
+            number = JT * b + j
             turned = bank("h_turned", [P, 2, P], number)
             for u in range(2):
-                nc.tensor.transpose(turned[:, u, :], h_rows[:].bitcast(F32)[:, u::2], ident[:])
-            grouped = ring.tile([P, PACK * P], BF16, name="h_g", align_bytes=64, bufs=3)
-            copy_out = nc.vector.tensor_copy if j < 2 else nc.scalar.copy
+                nc.tensor.transpose(turned[:, u, :], h_rows[b, j][:].bitcast(F32)[:, u::2], ident[:])
+            grouped = ring.tile([P, PACK * P], BF16, name="h_g", align_bytes=64, bufs=8)
             copy_out(
                 grouped[:].bitcast(F32).rearrange("p (j u) -> p j u", u=2),
                 turned[:].rearrange("p u j -> p j u"),
             )
-            h_q[b, j] = quantize("h%d%d" % (b, j), grouped[:], P)
+            codes = held("h%d%d_c" % (b, j), [P, P], U32)
+            scales = held("h%d%d_s" % (b, j), [P, P], U8)
+            nc.vector.quantize_mx(out=codes[:].bitcast(FP8X4), scales=scales[:], in_=grouped[:])
+            h_q[b, j] = codes, scales
 
-        def out_tile(j):
+        def out_tile(j, copy_out):
             res = bank("res", [P, JT, P], j)
             for b in range(PASSES):
                 for n in range(JT):
@@ -279,13 +309,20 @@ def tile_list_ocean_colour_gradient_kernel(
                         stop=(b == PASSES - 1 and n == JT - 1),
                     )
             staged = ring.tile([P, JT, P], F32, name="staged", bufs=JT)
-            copy_out = nc.vector.tensor_copy if j < 2 else nc.scalar.copy
             copy_out(staged[:], res[:])
             nc.sync.dma_start(out_rows[:, :, P * j : P * (j + 1)], staged[:])
 
-        for h in range(2):
-            for b in range(PASSES):
-                for j in (2 * h, 2 * h + 1):
-                    h_tile(b, j)
         for j in range(JT):
-            out_tile(j)
+            a_tile(0, j)
+            square_tile(0, j, square_on_scalar)
+        for j in range(JT):
+            a_tile(1, j)
+        for j in range(JT):
+            h_product(0, j)
+            h_turn(0, j, on_scalar)
+        for j in range(JT):
+            square_tile(1, j, square_on_scalar)
+            h_product(1, j)
+            h_turn(1, j, on_scalar)
+        for j in range(JT):
+            out_tile(j, on_vector if j % 2 else on_scalar)

@@ -91,26 +91,34 @@ def tile_list_ocean_colour_gradient_kernel(
             words = w3_words[0].rearrange("p n t -> p (n t)").bitcast(I32)
             nc.sync.dma_start(w3_w[b][:].bitcast(I32), words[:, KP * b : KP * (b + 1)])
 
+        def load_table_scales():
+            rows = tab_scales.rearrange("a (q r) n -> r q a n", r=4).bitcast(I32)
+            for r in range(4):
+                nc.sync.dma_start(tab_s[r:P:16, :].bitcast(I32), rows[r])
+
+        def load_w1_scales():
+            rows = w1_scales.rearrange("a (q r) y -> r q a y", r=4).bitcast(I32)
+            for r in range(4):
+                nc.sync.dma_start(w1_s[r:P:32].bitcast(I32), rows[r])
+
+        def load_w3_scales():
+            rows = w3_scales[0].rearrange("(q r) y -> r q y", r=4).bitcast(I32)
+            for r in range(4):
+                nc.sync.dma_start(w3_s[r:P:32, :].bitcast(I32), rows[r])
+
         load_plane(0, 0)
         nc.sync.dma_start(idx3[:], offs3)
         nc.sync.dma_start(idx2[:], offs2)
         load_plane(0, 1)
-        for a in range(PASSES):
-            for q in range(QUADS):
-                row = 32 * q + 4 * a
-                nc.sync.dma_start(tab_s[row : row + 4, :].bitcast(I32), tab_scales[a, 4 * q : 4 * q + 4, :].bitcast(I32))
-            load_plane(0, 2 + a)
-        for q in range(QUADS):
-            nc.sync.dma_start(
-                w1_s[32 * q : 32 * q + 4].bitcast(I32),
-                w1_scales[:, 4 * q : 4 * q + 4, :].rearrange("a r y -> r a y").bitcast(I32),
-            )
-        load_plane(1, 0)
-        for q in range(QUADS):
-            nc.sync.dma_start(w3_s[32 * q : 32 * q + 4, :].bitcast(I32), w3_scales[0, 4 * q : 4 * q + 4, :].bitcast(I32))
+        load_table_scales()
+        load_plane(0, 2)
+        load_w1_scales()
+        load_plane(0, 3)
+        load_w3_scales()
         nc.sync.dma_start(idx[:], offs)
         nc.vector.tensor_copy(v_s[0][:], tab_s[:].indirect(idx[:]))
-        nc.scalar.dma_start(v_s[1][0:100, :].bitcast(I32), v_s[0][4:104, :].bitcast(I32))
+        nc.scalar.dma_start(v_s[1][0:100, :].bitcast(I32), v_s[0][16:116, :].bitcast(I32))
+        load_plane(1, 0)
         load_plane(1, 1)
         load_plane(1, 2)
         load_w2(0, 0)

@@ -54,6 +54,10 @@ def tile_list_ocean_colour_gradient_kernel(
         w3_s = held("w3_s", [P, K], U8)
         w2_raw = [[held("w2_raw%d%d" % (a, b), [P, PACK, KP], F32) for b in range(PASSES)] for a in range(PASSES)]
         adj_raw = [held("adj_raw%d" % h, [P, PACK, HALF], F32) for h in range(2)]
+        w1_wp = [held("w1_wp%d" % b, [P, PASSES, 2 * KP], U8) for b in range(PASSES)]
+        w1_sp = held("w1_sp", [P, PASSES * K], U8)
+        w3_wp = [held("w3_wp%d" % b, [P, KP], U32) for b in range(PASSES)]
+        w3_sp = held("w3_sp", [P, K], U8)
         ident = held("ident", [P, P], F32)
         warm = held("warm", [P, 1], F32)
 
@@ -120,10 +124,10 @@ def tile_list_ocean_colour_gradient_kernel(
         nc.scalar.dma_start(v_s[1][0:100, :].bitcast(I32), v_s[0][16:116, :].bitcast(I32))
         load_plane(1, 0)
         load_plane(1, 1)
-        load_plane(1, 2)
         load_w2(0, 0)
-        load_plane(1, 3)
+        load_plane(1, 2)
         load_w2(1, 0)
+        load_plane(1, 3)
         load_w1(0)
         load_table(0)
         load_table(1)
@@ -201,6 +205,21 @@ def tile_list_ocean_colour_gradient_kernel(
                 nc.vector.quantize_mx(out=codes[:, cols].bitcast(FP8X4), scales=scales[:, cols], in_=grouped[:])
             return codes, scales
 
+        def x_pass_fused(a, codes_place):
+            diff = [held("diff%d" % h, [P, PACK, HALF], F32, place_of="plane0%d" % (2 + h)) for h in range(2)]
+            for t in range(PACK):
+                subtrahend = [ring.tile([P, HALF], F32, name="subtrahend%d" % h) for h in range(2)]
+                for h in range(2):
+                    nc.vector.tensor_copy(subtrahend[h][:], planes[a][t][:].indirect(idx3[:, 16 * h : 16 * (h + 1)]))
+                for h in range(2):
+                    nc.vector.tensor_tensor(
+                        diff[h][:, t, :],
+                        planes[a][t][:].indirect(idx2[:, 16 * h : 16 * (h + 1)]),
+                        subtrahend[h][:],
+                        ALU.subtract,
+                    )
+            return round_and_quantize("x%d" % a, [diff[0][:], diff[1][:]], [nc.scalar.copy] * 2, codes_place)
+
         on_scalar, on_vector = nc.scalar.copy, nc.vector.tensor_copy
 
         def gather_table(a):
@@ -210,96 +229,118 @@ def tile_list_ocean_colour_gradient_kernel(
             return words
 
         def prepare_w2(a, b, round_copies, codes_place=None):
-            return round_and_quantize("w2_%d%d" % (a, b), halves(w2_raw[a][b][:]), round_copies, codes_place)
+            grouped = held("w2_g%d%d" % (a, b), [P, PACK * KP], BF16)
+            dst = grouped[:].rearrange("p (t m k) -> p m k t", t=PACK, k=PACK)
+            src = w2_raw[a][b][:].rearrange("p k (m t) -> p m k t", t=PACK)
+            part = P // len(round_copies)
+            for i, round_copy in enumerate(round_copies):
+                round_copy(dst[:, part * i : part * (i + 1)], src[:, part * i : part * (i + 1)])
+            codes = held("w2_c%d%d" % (a, b), [P, KP], U32, place_of=codes_place)
+            scales = held("w2_s%d%d" % (a, b), [P, KP], U8)
+            nc.vector.quantize_mx(out=codes[:].bitcast(FP8X4), scales=scales[:], in_=grouped[:])
+            return codes, scales
+
+        def deal_scales(dst, src):
+            nc.vector.tensor_copy(
+                dst.rearrange("p (g t m) -> p g t m", t=PACK, m=P), src.rearrange("p (g m t) -> p g t m", t=PACK, m=P)
+            )
+
+        def deal_w1(b):
+            nc.vector.tensor_copy(
+                w1_wp[b][:].bitcast(U16).rearrange("p a (t m) -> p a t m", t=PACK),
+                w1_w[b][:].bitcast(U16).rearrange("p a (m t) -> p a t m", t=PACK),
+            )
+
+        def deal_w3(b):
+            nc.vector.tensor_copy(
+                w3_wp[b][:].bitcast(I32).rearrange("p (t g i) -> p g t i", t=PACK, i=4),
+                w3_w[b][:].bitcast(I32).rearrange("p (g i t) -> p g t i", t=PACK, i=4),
+            )
 
         def prepare_adj(h):
             return round_and_quantize("adj%d" % h, halves(adj_raw[h][:]), [negate_on_vector] * 2)
 
         x_q = [x_pass(0, "plane11")]
-        w2_q = {(0, 0): prepare_w2(0, 0, [on_scalar] * 2, "plane13")}
-        w2_q[1, 0] = prepare_w2(1, 0, [on_vector] * 2)
+        deal_scales(w1_sp[:], w1_s[:].rearrange("p a y -> p (a y)"))
+        deal_scales(w3_sp[:], w3_s[:])
+        w2_q = {(0, 0): prepare_w2(0, 0, [on_scalar], "plane12")}
+        w2_q[1, 0] = prepare_w2(1, 0, [on_scalar], "plane13")
+        deal_w1(0)
         v_w = [gather_table(0)]
-        x_q.append(x_pass(1, "tab_w0"))
+        x_q.append(x_pass_fused(1, "tab_w0"))
         v_w.append(gather_table(1))
-        w2_q[0, 1] = prepare_w2(0, 1, [on_vector] * 2)
-        w2_q[1, 1] = prepare_w2(1, 1, [on_vector] * 2)
-        neg_adj_q = [prepare_adj(h) for h in range(2)]
+        w2_q[0, 1] = prepare_w2(0, 1, [on_vector])
+        deal_w1(1)
+        w2_q[1, 1] = prepare_w2(1, 1, [on_vector])
+        neg_adj_q = [prepare_adj(0)]
+        deal_w3(0)
+        neg_adj_q.append(prepare_adj(1))
+        deal_w3(1)
 
-        def square_on_scalar(dst, src):
-            nc.scalar.activation(dst, src, ACT.Square)
-
-        def square_on_vector(dst, src):
-            nc.vector.tensor_tensor(dst, src, src, ALU.mult)
-
-        def square_on_gpsimd(dst, src):
-            nc.gpsimd.tensor_tensor(dst, src, src, ALU.mult)
-
-        h_q = {}
-        th = {}
+        th = [held("th%d" % b, [P, PACK, S], F32, place_of="plane0%d" % b) for b in range(PASSES)]
         th2 = {}
-        h_rows = {}
-        th2_place = [["plane00", "plane01", "plane02", "plane03"], ["plane10", "plane12", "w2_raw10", "w2_raw00"]]
+        th2_place = [["plane02", "plane03", "plane10", "tab_s"], ["w2_raw00", "w2_raw10", "tab_w1", "w2_raw01"]]
+        h_g = {}
+        h_q = {}
         out_rows = out.rearrange("(n p) j -> p n j", p=P)
 
-        def a_tile(b, j):
-            r = slice(KP * b, KP * (b + 1))
-            cols = slice(P * j, P * (j + 1))
-            acc = bank("acc", [P, KP], JT * b + j)
+        def a_tile(b, t):
+            cols = slice(P * t, P * (t + 1))
+            acc = bank("acc", [P, S], PACK * b + t)
             table = [
-                (v_w[a][:, cols], v_s[a][:, cols], w1_w[b][:, a, :].bitcast(FP4X4), w1_s[:, a, r]) for a in range(PASSES)
-            ]
-            bands = [
-                (x_q[a][0][:, cols], x_q[a][1][:, cols], w2_q[a, b][0][:].bitcast(FP8X4), w2_q[a, b][1][:])
+                (
+                    w1_wp[b][:, a, 2 * P * t : 2 * P * (t + 1)].bitcast(FP4X4),
+                    w1_sp[:, K * a + KP * b + P * t : K * a + KP * b + P * (t + 1)],
+                    v_w[a],
+                    v_s[a],
+                )
                 for a in range(PASSES)
             ]
+            bands = [(w2_q[a, b][0][:, cols].bitcast(FP8X4), w2_q[a, b][1][:, cols], *x_q[a]) for a in range(PASSES)]
             passes = [bands[0], table[0], bands[1], table[1]] if b == 0 else table + bands
-            for i, (words, scale, rhs, rhs_scale) in enumerate(passes):
+            for i, (lhsT, lhsT_scale, words, scales) in enumerate(passes):
                 nc.tensor.matmul_mx(
                     out=acc[:],
-                    lhsT=words.bitcast(FP8X4),
-                    lhsT_scale=scale,
-                    rhs=rhs,
-                    rhs_scale=rhs_scale,
+                    lhsT=lhsT,
+                    lhsT_scale=lhsT_scale,
+                    rhs=words[:].bitcast(FP8X4),
+                    rhs_scale=scales[:],
                     start=(i == 0),
                     stop=(i == len(passes) - 1),
                 )
-            th[b, j] = ring.tile([P, KP], F32, name="th", bufs=JT)
-            nc.scalar.activation(th[b, j][:], acc[:], ACT.Tanh)
+            nc.scalar.activation(th[b][:, t, :], acc[:], ACT.Tanh)
 
-        def square_tile(b, j, square):
-            th2[b, j] = held("th2_%d%d" % (b, j), [P, KP], F32, place_of=th2_place[b][j])
-            square(th2[b, j][:], th[b, j][:])
+        def square_tile(b, j):
+            th2[b, j] = held("th2_%d%d" % (b, j), [P, PACK * P], F32, place_of=th2_place[b][j])
+            nc.scalar.activation(*group_views(th2[b, j][:], th[b][:, :, P * j : P * (j + 1)]), ACT.Square)
 
         def h_product(b, j):
-            number = JT * b + j
-            r = slice(KP * b, KP * (b + 1))
-            neg_e = bank("neg_e", [P, KP], number)
+            neg_e = bank("neg_e", [P, PACK, P], JT * b + j)
             adj_cols = slice(P * (j % 2), P * (j % 2 + 1))
-            nc.tensor.matmul_mx(
-                out=neg_e[:],
-                lhsT=neg_adj_q[j // 2][0][:, adj_cols].bitcast(FP8X4),
-                lhsT_scale=neg_adj_q[j // 2][1][:, adj_cols],
-                rhs=w3_w[b][:].bitcast(FP8X4),
-                rhs_scale=w3_s[:, r],
-                start=True,
-                stop=True,
+            for t in range(PACK):
+                nc.tensor.matmul_mx(
+                    out=neg_e[:, t, :],
+                    lhsT=w3_wp[b][:, P * t : P * (t + 1)].bitcast(FP8X4),
+                    lhsT_scale=w3_sp[:, KP * b + P * t : KP * b + P * (t + 1)],
+                    rhs=neg_adj_q[j // 2][0][:, adj_cols].bitcast(FP8X4),
+                    rhs_scale=neg_adj_q[j // 2][1][:, adj_cols],
+                    start=True,
+                    stop=True,
+                )
+            h_g[b, j] = held("h_g%d%d" % (b, j), [P, PACK * P], BF16)
+            nc.vector.scalar_tensor_tensor(
+                h_g[b, j][:].rearrange("p (c t) -> p c t", t=PACK),
+                th2[b, j][:].rearrange("p (c t) -> p c t", t=PACK),
+                1.0,
+                neg_e[:].rearrange("p t c -> p c t"),
+                ALU.subtract,
+                ALU.mult,
             )
-            h_rows[b, j] = held("h_rows%d%d" % (b, j), [P, KP], BF16)
-            nc.vector.scalar_tensor_tensor(h_rows[b, j][:], th2[b, j][:], 1.0, neg_e[:], ALU.subtract, ALU.mult)
 
-        def h_turn(b, j, copy_out):
-            number = JT * b + j
-            turned = bank("h_turned", [P, 2, P], number)
-            for u in range(2):
-                nc.tensor.transpose(turned[:, u, :], h_rows[b, j][:].bitcast(F32)[:, u::2], ident[:])
-            grouped = ring.tile([P, PACK * P], BF16, name="h_g", align_bytes=64, bufs=8)
-            copy_out(
-                grouped[:].bitcast(F32).rearrange("p (j u) -> p j u", u=2),
-                turned[:].rearrange("p u j -> p j u"),
-            )
+        def h_quantize(b, j):
             codes = held("h%d%d_c" % (b, j), [P, P], U32)
             scales = held("h%d%d_s" % (b, j), [P, P], U8)
-            nc.vector.quantize_mx(out=codes[:].bitcast(FP8X4), scales=scales[:], in_=grouped[:])
+            nc.vector.quantize_mx(out=codes[:].bitcast(FP8X4), scales=scales[:], in_=h_g[b, j][:])
             h_q[b, j] = codes, scales
 
         def out_tile(j, copy_out):
@@ -320,17 +361,16 @@ def tile_list_ocean_colour_gradient_kernel(
             copy_out(staged[:], res[:])
             nc.sync.dma_start(out_rows[:, :, P * j : P * (j + 1)], staged[:])
 
+        for b in range(PASSES):
+            for t in range(PACK):
+                a_tile(b, t)
+            for j in range(JT):
+                square_tile(b, j)
+        units = [(b, j) for b in range(PASSES) for j in range(JT)]
+        for i, unit in enumerate(units):
+            h_product(*unit)
+            if i > 0:
+                h_quantize(*units[i - 1])
+        h_quantize(*units[-1])
         for j in range(JT):
-            a_tile(0, j)
-            square_tile(0, j, square_on_scalar)
-        for j in range(JT):
-            a_tile(1, j)
-        for j in range(JT):
-            h_product(0, j)
-            h_turn(0, j, on_scalar)
-        for j in range(JT):
-            square_tile(1, j, square_on_scalar)
-            h_product(1, j)
-            h_turn(1, j, on_scalar)
-        for j in range(JT):
-            out_tile(j, on_vector if j % 2 else on_scalar)
+            out_tile(j, on_scalar)

@@ -51,19 +51,17 @@ def tile_list_ocean_colour_gradient_kernel(
         w1_w = [held("w1_w%d" % b, [P, PASSES, 2 * KP], U8) for b in range(PASSES)]
         w1_s = held("w1_s", [P, PASSES, K], U8)
         w3_w = [held("w3_w%d" % b, [P, KP], U32) for b in range(PASSES)]
-        w3_s = held("w3_s", [P, K], U8)
         w2_raw = [[held("w2_raw%d%d" % (a, b), [P, PACK, KP], F32) for b in range(PASSES)] for a in range(PASSES)]
         adj_raw = [held("adj_raw%d" % h, [P, PACK, HALF], F32) for h in range(2)]
         w1_wp = [held("w1_wp%d" % b, [P, PASSES, 2 * KP], U8) for b in range(PASSES)]
         w1_sp = held("w1_sp", [P, PASSES * K], U8)
         w3_wp = [held("w3_wp%d" % b, [P, KP], U32) for b in range(PASSES)]
-        w3_sp = held("w3_sp", [P, K], U8)
+        subtrahend = [[held("subtrahend%d%d" % (t, h), [P, HALF], F32) for h in range(2)] for t in range(PACK)]
         ident = held("ident", [P, P], F32)
         warm = held("warm", [P, 1], F32)
 
         nc.vector.memset(tab_s[:].bitcast(I32), 0)
         nc.vector.memset(w1_s[:].rearrange("p a t -> p (a t)").bitcast(I32), 0)
-        nc.vector.memset(w3_s[:].bitcast(I32), 0)
         nc.vector.memset(v_s[1][:].bitcast(I32), 0)
         make_identity(nc, ident[:])
         nc.scalar.activation(warm[:], ident[:, 0:1], ACT.Tanh)
@@ -100,15 +98,15 @@ def tile_list_ocean_colour_gradient_kernel(
             for r in range(4):
                 nc.sync.dma_start(tab_s[r:P:16, :].bitcast(I32), rows[r])
 
-        def load_w1_scales():
+        def load_w1_scales(first, last):
             rows = w1_scales.rearrange("a (q r) y -> r q a y", r=4).bitcast(I32)
-            for r in range(4):
+            for r in range(first, last):
                 nc.sync.dma_start(w1_s[r:P:32].bitcast(I32), rows[r])
 
         def load_w3_scales():
             rows = w3_scales[0].rearrange("(q r) y -> r q y", r=4).bitcast(I32)
             for r in range(4):
-                nc.sync.dma_start(w3_s[r:P:32, :].bitcast(I32), rows[r])
+                nc.sync.dma_start(w1_s[4 + r : P : 32, 0, :].bitcast(I32), rows[r])
 
         load_plane(0, 0)
         nc.sync.dma_start(idx3[:], offs3)
@@ -116,7 +114,7 @@ def tile_list_ocean_colour_gradient_kernel(
         load_plane(0, 1)
         load_table_scales()
         load_plane(0, 2)
-        load_w1_scales()
+        load_w1_scales(0, 4)
         load_plane(0, 3)
         load_w3_scales()
         nc.sync.dma_start(idx[:], offs)
@@ -134,8 +132,8 @@ def tile_list_ocean_colour_gradient_kernel(
         load_w2(0, 1)
         load_w1(1)
         load_w2(1, 1)
-        load_adj(0)
         load_w3(0)
+        load_adj(0)
         load_adj(1)
         load_w3(1)
 
@@ -166,7 +164,7 @@ def tile_list_ocean_colour_gradient_kernel(
         def negate_on_vector(dst, src):
             nc.vector.tensor_scalar(dst, src, -1.0, None, ALU.mult)
 
-        def x_pass(a, codes_place):
+        def x_pass(a):
             turned = []
             for u in range(2):
                 sums = [bank("x_sum", [P, 2, 2, P], 4 + 2 * u + h) for h in range(2)]
@@ -193,39 +191,43 @@ def tile_list_ocean_colour_gradient_kernel(
                         turned.append(bank("x_turned", [P, 2, 2, P], 4 + h))
                     for j in range(2):
                         nc.tensor.transpose(turned[h][:, j, u, :], pairs[:, j, :].bitcast(F32), ident[:])
-            codes = held("x%d_c" % a, [P, S], U32, place_of=codes_place)
-            scales = held("x%d_s" % a, [P, S], U8)
+            parts = []
             for h in range(2):
                 grouped = ring.tile([P, PACK * HALF], BF16, name="x_g", align_bytes=64)
                 nc.scalar.copy(
                     grouped[:].bitcast(F32).rearrange("p (j m u) -> p j m u", j=2, u=2),
                     turned[h][:].rearrange("p j u m -> p j m u"),
                 )
+                parts.append(grouped)
+            return parts
+
+        def quantize_parts(name, parts, codes_place):
+            codes = held(name + "_c", [P, S], U32, place_of=codes_place)
+            scales = held(name + "_s", [P, S], U8)
+            for h, grouped in enumerate(parts):
                 cols = slice(HALF * h, HALF * (h + 1))
                 nc.vector.quantize_mx(out=codes[:, cols].bitcast(FP8X4), scales=scales[:, cols], in_=grouped[:])
             return codes, scales
 
-        def x_pass_fused(a, codes_place):
+        def x_pass_fused(a):
             diff = [held("diff%d" % h, [P, PACK, HALF], F32, place_of="plane0%d" % (2 + h)) for h in range(2)]
             for t in range(PACK):
-                subtrahend = [ring.tile([P, HALF], F32, name="subtrahend%d" % h) for h in range(2)]
                 for h in range(2):
-                    nc.vector.tensor_copy(subtrahend[h][:], planes[a][t][:].indirect(idx3[:, 16 * h : 16 * (h + 1)]))
+                    nc.vector.tensor_copy(subtrahend[t][h][:], planes[a][t][:].indirect(idx3[:, 16 * h : 16 * (h + 1)]))
                 for h in range(2):
                     nc.vector.tensor_tensor(
                         diff[h][:, t, :],
                         planes[a][t][:].indirect(idx2[:, 16 * h : 16 * (h + 1)]),
-                        subtrahend[h][:],
+                        subtrahend[t][h][:],
                         ALU.subtract,
                     )
-            return round_and_quantize("x%d" % a, [diff[0][:], diff[1][:]], [nc.scalar.copy] * 2, codes_place)
+            return diff
 
         on_scalar, on_vector = nc.scalar.copy, nc.vector.tensor_copy
 
         def gather_table(a):
             words = held("v_w%d" % a, [P, S], U32)
-            for h in range(2):
-                nc.vector.tensor_copy(words[:, HALF * h : HALF * (h + 1)], tab_w[a][:].indirect(idx[:, 16 * h : 16 * (h + 1)]))
+            nc.vector.tensor_copy(words[:], tab_w[a][:].indirect(idx[:]))
             return words
 
         def prepare_w2(a, b, round_copies, codes_place=None):
@@ -260,20 +262,21 @@ def tile_list_ocean_colour_gradient_kernel(
         def prepare_adj(h):
             return round_and_quantize("adj%d" % h, halves(adj_raw[h][:]), [negate_on_vector] * 2)
 
-        x_q = [x_pass(0, "plane11")]
+        x0_parts = x_pass(0)
+        diff = x_pass_fused(1)
+        x_q = [quantize_parts("x0", x0_parts, "subtrahend10")]
         deal_scales(w1_sp[:], w1_s[:].rearrange("p a y -> p (a y)"))
-        deal_scales(w3_sp[:], w3_s[:])
-        w2_q = {(0, 0): prepare_w2(0, 0, [on_scalar], "plane12")}
-        w2_q[1, 0] = prepare_w2(1, 0, [on_scalar], "plane13")
+        w2_q = {(0, 0): prepare_w2(0, 0, [on_scalar], "subtrahend20")}
+        w2_q[1, 0] = prepare_w2(1, 0, [on_scalar], "subtrahend30")
         deal_w1(0)
         v_w = [gather_table(0)]
-        x_q.append(x_pass_fused(1, "tab_w0"))
+        x_q.append(round_and_quantize("x1", [diff[0][:], diff[1][:]], [on_scalar] * 2))
         v_w.append(gather_table(1))
         w2_q[0, 1] = prepare_w2(0, 1, [on_vector])
         deal_w1(1)
         w2_q[1, 1] = prepare_w2(1, 1, [on_vector])
-        neg_adj_q = [prepare_adj(0)]
         deal_w3(0)
+        neg_adj_q = [prepare_adj(0)]
         neg_adj_q.append(prepare_adj(1))
         deal_w3(1)
 
@@ -321,7 +324,7 @@ def tile_list_ocean_colour_gradient_kernel(
                 nc.tensor.matmul_mx(
                     out=neg_e[:, t, :],
                     lhsT=w3_wp[b][:, P * t : P * (t + 1)].bitcast(FP8X4),
-                    lhsT_scale=w3_sp[:, KP * b + P * t : KP * b + P * (t + 1)],
+                    lhsT_scale=w1_sp[4:, KP * b + P * t : KP * b + P * (t + 1)],
                     rhs=neg_adj_q[j // 2][0][:, adj_cols].bitcast(FP8X4),
                     rhs_scale=neg_adj_q[j // 2][1][:, adj_cols],
                     start=True,
@@ -343,11 +346,11 @@ def tile_list_ocean_colour_gradient_kernel(
             nc.vector.quantize_mx(out=codes[:].bitcast(FP8X4), scales=scales[:], in_=h_g[b, j][:])
             h_q[b, j] = codes, scales
 
-        def out_tile(j, copy_out):
-            res = bank("res", [P, JT, P], j)
+        def out_rows_of(j, first, count, number, copy_out):
+            res = bank("res", [P, count, P], number)
             for b in range(PASSES):
-                for n in range(JT):
-                    cols = slice(P * n, P * (n + 1))
+                for n in range(count):
+                    cols = slice(P * (first + n), P * (first + n + 1))
                     nc.tensor.matmul_mx(
                         out=res[:, n, :],
                         lhsT=v_w[b][:, cols].bitcast(FP8X4),
@@ -355,22 +358,24 @@ def tile_list_ocean_colour_gradient_kernel(
                         rhs=h_q[b, j][0][:].bitcast(FP8X4),
                         rhs_scale=h_q[b, j][1][:],
                         start=(b == 0 and n == 0),
-                        stop=(b == PASSES - 1 and n == JT - 1),
+                        stop=(b == PASSES - 1 and n == count - 1),
                     )
-            staged = ring.tile([P, JT, P], F32, name="staged", bufs=JT)
+            staged = held("staged%d%d" % (j, first), [P, count, P], F32)
             copy_out(staged[:], res[:])
-            nc.sync.dma_start(out_rows[:, :, P * j : P * (j + 1)], staged[:])
+            nc.sync.dma_start(out_rows[:, first : first + count, P * j : P * (j + 1)], staged[:])
 
         for b in range(PASSES):
             for t in range(PACK):
                 a_tile(b, t)
             for j in range(JT):
                 square_tile(b, j)
-        units = [(b, j) for b in range(PASSES) for j in range(JT)]
+        units = [(b, j) for b in range(PASSES) for j in range(JT - 1)] + [(b, JT - 1) for b in range(PASSES)]
         for i, unit in enumerate(units):
             h_product(*unit)
             if i > 0:
                 h_quantize(*units[i - 1])
         h_quantize(*units[-1])
-        for j in range(JT):
-            out_tile(j, on_scalar)
+        for j in range(JT - 1):
+            out_rows_of(j, 0, JT, j, on_scalar)
+        out_rows_of(JT - 1, 0, 2, JT - 1, on_vector)
+        out_rows_of(JT - 1, 2, 2, JT, on_scalar)

@@ -23,7 +23,13 @@ KP = P * PACK
 PASSES = K // KP
 JT = S // P
 HALF = S // 2
-QUADS = 4
+LIST_COLS = S // 16
+QUAD = 32
+ROWS = 4
+TAB_SHIFT = 16
+W3_SHIFT = 4
+SCALE_SPAN = 3 * QUAD + ROWS
+X_BANK = 4
 
 
 def tile_list_ocean_colour_gradient_kernel(
@@ -41,30 +47,28 @@ def tile_list_ocean_colour_gradient_kernel(
         def bank(name, shape, number):
             return psum.tile(shape, F32, name=name, tag="bank%d" % number)
 
-        idx = keep.tile([P, S // 16], U16, name="idx")
-        idx2 = keep.tile([P, S // 16], U16, name="idx2")
-        idx3 = keep.tile([P, S // 16], U16, name="idx3")
+        idx = keep.tile([P, LIST_COLS], U16, name="idx")
+        idx2 = keep.tile([P, LIST_COLS], U16, name="idx2")
+        idx3 = keep.tile([P, LIST_COLS], U16, name="idx3")
         planes = [[held("plane%d%d" % (a, t), [P, T], F32) for t in range(PACK)] for a in range(PASSES)]
         tab_w = [held("tab_w%d" % a, [P, T], U32) for a in range(PASSES)]
         tab_s = held("tab_s", [P, T], U8)
         v_s = [held("v_s%d" % a, [P, S], U8) for a in range(PASSES)]
         w1_w = [held("w1_w%d" % b, [P, PASSES, 2 * KP], U8) for b in range(PASSES)]
-        w1_s = held("w1_s", [P, PASSES, K], U8)
+        weight_s = held("weight_s", [P, PASSES, K], U8)
         w3_w = [held("w3_w%d" % b, [P, KP], U32) for b in range(PASSES)]
         w2_raw = [[held("w2_raw%d%d" % (a, b), [P, PACK, KP], F32) for b in range(PASSES)] for a in range(PASSES)]
         adj_raw = [held("adj_raw%d" % h, [P, PACK, HALF], F32) for h in range(2)]
-        w1_wp = [held("w1_wp%d" % b, [P, PASSES, 2 * KP], U8) for b in range(PASSES)]
-        w1_sp = held("w1_sp", [P, PASSES * K], U8)
-        w3_wp = [held("w3_wp%d" % b, [P, KP], U32) for b in range(PASSES)]
+        w1_dealt = [held("w1_dealt%d" % b, [P, PASSES, 2 * KP], U8) for b in range(PASSES)]
+        weight_s_dealt = held("weight_s_dealt", [P, PASSES * K], U8)
+        w3_dealt = [held("w3_dealt%d" % b, [P, KP], U32) for b in range(PASSES)]
         subtrahend = [[held("subtrahend%d%d" % (t, h), [P, HALF], F32) for h in range(2)] for t in range(PACK)]
         ident = held("ident", [P, P], F32)
-        warm = held("warm", [P, 1], F32)
 
         nc.vector.memset(tab_s[:].bitcast(I32), 0)
-        nc.vector.memset(w1_s[:].rearrange("p a t -> p (a t)").bitcast(I32), 0)
+        nc.vector.memset(weight_s[:].rearrange("p a r -> p (a r)").bitcast(I32), 0)
         nc.vector.memset(v_s[1][:].bitcast(I32), 0)
         make_identity(nc, ident[:])
-        nc.scalar.activation(warm[:], ident[:, 0:1], ACT.Tanh)
 
         x_rows = xT.rearrange("(a p t) c -> a t p c", a=PASSES, t=PACK)
 
@@ -87,26 +91,27 @@ def tile_list_ocean_colour_gradient_kernel(
             )
 
         def load_adj(h):
-            nc.sync.dma_start(adj_raw[h][:], adj.rearrange("(p t) c -> p t c", t=PACK)[:, :, HALF * h : HALF * (h + 1)])
+            rows = adj.rearrange("(p t) c -> p t c", t=PACK)
+            nc.sync.dma_start(adj_raw[h][:], rows[:, :, HALF * h : HALF * (h + 1)])
 
         def load_w3(b):
             words = w3_words[0].rearrange("p n t -> p (n t)").bitcast(I32)
             nc.sync.dma_start(w3_w[b][:].bitcast(I32), words[:, KP * b : KP * (b + 1)])
 
         def load_table_scales():
-            rows = tab_scales.rearrange("a (q r) n -> r q a n", r=4).bitcast(I32)
-            for r in range(4):
-                nc.sync.dma_start(tab_s[r:P:16, :].bitcast(I32), rows[r])
+            rows = tab_scales.rearrange("a (q i) n -> i q a n", i=ROWS).bitcast(I32)
+            for i in range(ROWS):
+                nc.sync.dma_start(tab_s[i:P:TAB_SHIFT, :].bitcast(I32), rows[i])
 
-        def load_w1_scales(first, last):
-            rows = w1_scales.rearrange("a (q r) y -> r q a y", r=4).bitcast(I32)
-            for r in range(first, last):
-                nc.sync.dma_start(w1_s[r:P:32].bitcast(I32), rows[r])
+        def load_w1_scales():
+            rows = w1_scales.rearrange("a (q i) y -> i q a y", i=ROWS).bitcast(I32)
+            for i in range(ROWS):
+                nc.sync.dma_start(weight_s[i:P:QUAD].bitcast(I32), rows[i])
 
         def load_w3_scales():
-            rows = w3_scales[0].rearrange("(q r) y -> r q y", r=4).bitcast(I32)
-            for r in range(4):
-                nc.sync.dma_start(w1_s[4 + r : P : 32, 0, :].bitcast(I32), rows[r])
+            rows = w3_scales[0].rearrange("(q i) y -> i q y", i=ROWS).bitcast(I32)
+            for i in range(ROWS):
+                nc.sync.dma_start(weight_s[W3_SHIFT + i : P : QUAD, 0, :].bitcast(I32), rows[i])
 
         load_plane(0, 0)
         nc.sync.dma_start(idx3[:], offs3)
@@ -114,12 +119,14 @@ def tile_list_ocean_colour_gradient_kernel(
         load_plane(0, 1)
         load_table_scales()
         load_plane(0, 2)
-        load_w1_scales(0, 4)
+        load_w1_scales()
         load_plane(0, 3)
         load_w3_scales()
         nc.sync.dma_start(idx[:], offs)
         nc.vector.tensor_copy(v_s[0][:], tab_s[:].indirect(idx[:]))
-        nc.scalar.dma_start(v_s[1][0:100, :].bitcast(I32), v_s[0][16:116, :].bitcast(I32))
+        nc.scalar.dma_start(
+            v_s[1][0:SCALE_SPAN, :].bitcast(I32), v_s[0][TAB_SHIFT : TAB_SHIFT + SCALE_SPAN, :].bitcast(I32)
+        )
         load_plane(1, 0)
         load_plane(1, 1)
         load_w2(0, 0)
@@ -129,8 +136,8 @@ def tile_list_ocean_colour_gradient_kernel(
         load_w1(0)
         load_table(0)
         load_table(1)
-        load_w2(0, 1)
         load_w1(1)
+        load_w2(0, 1)
         load_w2(1, 1)
         load_w3(0)
         load_adj(0)
@@ -143,33 +150,29 @@ def tile_list_ocean_colour_gradient_kernel(
                 raw.rearrange("p t (c i) -> p c t i", i=4),
             )
 
-        def round_and_quantize(name, parts, round_copies, codes_place=None):
-            width = parts[0].shape[2]
+        def quantize(name, parts, codes_place=None):
+            width = parts[0][:].shape[1] // PACK
             codes = held(name + "_c", [P, width * len(parts)], U32, place_of=codes_place)
             scales = held(name + "_s", [P, width * len(parts)], U8)
-            grouped = []
-            for i, raw in enumerate(parts):
-                tile = held("%s_g%d" % (name, i), [P, PACK * width], BF16)
-                round_copies[i](*group_views(tile[:], raw))
-                grouped.append(tile)
-            for i, tile in enumerate(grouped):
+            for i, grouped in enumerate(parts):
                 cols = slice(width * i, width * (i + 1))
-                nc.vector.quantize_mx(out=codes[:, cols].bitcast(FP8X4), scales=scales[:, cols], in_=tile[:])
+                nc.vector.quantize_mx(out=codes[:, cols].bitcast(FP8X4), scales=scales[:, cols], in_=grouped[:])
             return codes, scales
 
-        def halves(raw):
-            width = raw.shape[2] // 2
-            return [raw[:, :, width * h : width * (h + 1)] for h in range(2)]
+        def round_parts(name, parts, round_copy):
+            tiles = []
+            for i, raw in enumerate(parts):
+                grouped = held("%s_g%d" % (name, i), [P, PACK * raw.shape[2]], BF16)
+                round_copy(*group_views(grouped[:], raw))
+                tiles.append(grouped)
+            return tiles
 
-        def negate_on_vector(dst, src):
-            nc.vector.tensor_scalar(dst, src, -1.0, None, ALU.mult)
-
-        def x_pass(a):
+        def x_by_transposes(a):
             turned = []
             for u in range(2):
-                sums = [bank("x_sum", [P, 2, 2, P], 4 + 2 * u + h) for h in range(2)]
-                for e in range(2):
-                    plane = planes[a][2 * u + e]
+                sums = [bank("x_sum", [P, 2, 2, P], X_BANK + 2 * u + h) for h in range(2)]
+                for odd in range(2):
+                    plane = planes[a][2 * u + odd]
                     plus = ring.tile([P, S], F32, name="plus")
                     minus = ring.tile([P, S], F32, name="minus")
                     picked = ring.tile([P, S], F32, name="picked")
@@ -178,122 +181,115 @@ def tile_list_ocean_colour_gradient_kernel(
                     nc.vector.tensor_copy(plus[:], plane[:].indirect(idx2[:]))
                     for j in range(JT):
                         cols = slice(P * j, P * (j + 1))
-                        dst = sums[j // 2][:, j % 2, e, :]
+                        dst = sums[j // 2][:, j % 2, odd, :]
                         nc.tensor.matmul(dst, minus[:, cols], ident[:], start=True, stop=False, is_transpose=True)
                         nc.tensor.matmul(dst, plus[:, cols], ident[:], start=False, stop=True, is_transpose=True)
                 for h in range(2):
                     pairs = ring.tile([P, 2, 2 * P], BF16, name="x_pairs", align_bytes=64)
                     nc.scalar.copy(
-                        pairs[:].rearrange("p j (m e) -> p j m e", e=2),
-                        sums[h][:].rearrange("p j e m -> p j m e"),
+                        pairs[:].rearrange("p i (m odd) -> p i m odd", odd=2),
+                        sums[h][:].rearrange("p i odd m -> p i m odd"),
                     )
                     if u == 0:
-                        turned.append(bank("x_turned", [P, 2, 2, P], 4 + h))
-                    for j in range(2):
-                        nc.tensor.transpose(turned[h][:, j, u, :], pairs[:, j, :].bitcast(F32), ident[:])
+                        turned.append(bank("x_turned", [P, 2, 2, P], X_BANK + h))
+                    for i in range(2):
+                        nc.tensor.transpose(turned[h][:, i, u, :], pairs[:, i, :].bitcast(F32), ident[:])
             parts = []
             for h in range(2):
                 grouped = ring.tile([P, PACK * HALF], BF16, name="x_g", align_bytes=64)
                 nc.scalar.copy(
-                    grouped[:].bitcast(F32).rearrange("p (j m u) -> p j m u", j=2, u=2),
-                    turned[h][:].rearrange("p j u m -> p j m u"),
+                    grouped[:].bitcast(F32).rearrange("p (i m u) -> p i m u", i=2, u=2),
+                    turned[h][:].rearrange("p i u m -> p i m u"),
                 )
                 parts.append(grouped)
             return parts
 
-        def quantize_parts(name, parts, codes_place):
-            codes = held(name + "_c", [P, S], U32, place_of=codes_place)
-            scales = held(name + "_s", [P, S], U8)
-            for h, grouped in enumerate(parts):
-                cols = slice(HALF * h, HALF * (h + 1))
-                nc.vector.quantize_mx(out=codes[:, cols].bitcast(FP8X4), scales=scales[:, cols], in_=grouped[:])
-            return codes, scales
-
-        def x_pass_fused(a):
+        def x_by_subtraction(a):
             diff = [held("diff%d" % h, [P, PACK, HALF], F32, place_of="plane0%d" % (2 + h)) for h in range(2)]
+            offsets = [slice(LIST_COLS // 2 * h, LIST_COLS // 2 * (h + 1)) for h in range(2)]
             for t in range(PACK):
                 for h in range(2):
-                    nc.vector.tensor_copy(subtrahend[t][h][:], planes[a][t][:].indirect(idx3[:, 16 * h : 16 * (h + 1)]))
+                    nc.vector.tensor_copy(subtrahend[t][h][:], planes[a][t][:].indirect(idx3[:, offsets[h]]))
                 for h in range(2):
                     nc.vector.tensor_tensor(
                         diff[h][:, t, :],
-                        planes[a][t][:].indirect(idx2[:, 16 * h : 16 * (h + 1)]),
+                        planes[a][t][:].indirect(idx2[:, offsets[h]]),
                         subtrahend[t][h][:],
                         ALU.subtract,
                     )
-            return diff
-
-        on_scalar, on_vector = nc.scalar.copy, nc.vector.tensor_copy
+            return [diff[h][:] for h in range(2)]
 
         def gather_table(a):
             words = held("v_w%d" % a, [P, S], U32)
             nc.vector.tensor_copy(words[:], tab_w[a][:].indirect(idx[:]))
             return words
 
-        def prepare_w2(a, b, round_copies, codes_place=None):
+        def prepare_w2(a, b, round_copy, codes_place=None):
             grouped = held("w2_g%d%d" % (a, b), [P, PACK * KP], BF16)
-            dst = grouped[:].rearrange("p (t m k) -> p m k t", t=PACK, k=PACK)
-            src = w2_raw[a][b][:].rearrange("p k (m t) -> p m k t", t=PACK)
-            part = P // len(round_copies)
-            for i, round_copy in enumerate(round_copies):
-                round_copy(dst[:, part * i : part * (i + 1)], src[:, part * i : part * (i + 1)])
-            codes = held("w2_c%d%d" % (a, b), [P, KP], U32, place_of=codes_place)
-            scales = held("w2_s%d%d" % (a, b), [P, KP], U8)
-            nc.vector.quantize_mx(out=codes[:].bitcast(FP8X4), scales=scales[:], in_=grouped[:])
-            return codes, scales
+            round_copy(
+                grouped[:].rearrange("p (t m i) -> p m i t", t=PACK, i=PACK),
+                w2_raw[a][b][:].rearrange("p i (m t) -> p m i t", t=PACK),
+            )
+            return quantize("w2_%d%d" % (a, b), [grouped], codes_place)
 
-        def deal_scales(dst, src):
+        def deal_scales():
             nc.vector.tensor_copy(
-                dst.rearrange("p (g t m) -> p g t m", t=PACK, m=P), src.rearrange("p (g m t) -> p g t m", t=PACK, m=P)
+                weight_s_dealt[:].rearrange("p (g t m) -> p g t m", t=PACK, m=P),
+                weight_s[:].rearrange("p a r -> p (a r)").rearrange("p (g m t) -> p g t m", t=PACK, m=P),
             )
 
         def deal_w1(b):
             nc.vector.tensor_copy(
-                w1_wp[b][:].bitcast(U16).rearrange("p a (t m) -> p a t m", t=PACK),
+                w1_dealt[b][:].bitcast(U16).rearrange("p a (t m) -> p a t m", t=PACK),
                 w1_w[b][:].bitcast(U16).rearrange("p a (m t) -> p a t m", t=PACK),
             )
 
         def deal_w3(b):
             nc.vector.tensor_copy(
-                w3_wp[b][:].bitcast(I32).rearrange("p (t g i) -> p g t i", t=PACK, i=4),
+                w3_dealt[b][:].bitcast(I32).rearrange("p (t g i) -> p g t i", t=PACK, i=4),
                 w3_w[b][:].bitcast(I32).rearrange("p (g i t) -> p g t i", t=PACK, i=4),
             )
 
-        def prepare_adj(h):
-            return round_and_quantize("adj%d" % h, halves(adj_raw[h][:]), [negate_on_vector] * 2)
+        def negate_on_vector(dst, src):
+            nc.vector.tensor_scalar(dst, src, -1.0, None, ALU.mult)
 
-        x0_parts = x_pass(0)
-        diff = x_pass_fused(1)
-        x_q = [quantize_parts("x0", x0_parts, "subtrahend10")]
-        deal_scales(w1_sp[:], w1_s[:].rearrange("p a y -> p (a y)"))
-        w2_q = {(0, 0): prepare_w2(0, 0, [on_scalar], "subtrahend20")}
-        w2_q[1, 0] = prepare_w2(1, 0, [on_scalar], "subtrahend30")
+        def prepare_neg_adj(h):
+            parts = [adj_raw[h][:, :, P * i : P * (i + 1)] for i in range(2)]
+            return quantize("adj%d" % h, round_parts("adj%d" % h, parts, negate_on_vector))
+
+        on_scalar, on_vector = nc.scalar.copy, nc.vector.tensor_copy
+
+        x0_grouped = x_by_transposes(0)
+        x1_float = x_by_subtraction(1)
+        x_q = [quantize("x0", x0_grouped, "subtrahend10")]
+        deal_scales()
+        w2_q = {(0, 0): prepare_w2(0, 0, on_scalar, "subtrahend30")}
+        w2_q[1, 0] = prepare_w2(1, 0, on_scalar, "subtrahend31")
         deal_w1(0)
         v_w = [gather_table(0)]
-        x_q.append(round_and_quantize("x1", [diff[0][:], diff[1][:]], [on_scalar] * 2))
+        x_q.append(quantize("x1", round_parts("x1", x1_float, on_scalar)))
         v_w.append(gather_table(1))
-        w2_q[0, 1] = prepare_w2(0, 1, [on_vector])
         deal_w1(1)
-        w2_q[1, 1] = prepare_w2(1, 1, [on_vector])
+        w2_q[0, 1] = prepare_w2(0, 1, on_vector)
+        w2_q[1, 1] = prepare_w2(1, 1, on_vector)
         deal_w3(0)
-        neg_adj_q = [prepare_adj(0)]
-        neg_adj_q.append(prepare_adj(1))
+        neg_adj_q = [prepare_neg_adj(h) for h in range(2)]
         deal_w3(1)
 
         th = [held("th%d" % b, [P, PACK, S], F32, place_of="plane0%d" % b) for b in range(PASSES)]
-        th2 = {}
         th2_place = [["plane02", "plane03", "plane10", "tab_s"], ["w2_raw00", "w2_raw10", "tab_w1", "w2_raw01"]]
-        h_g = {}
+        th2 = {}
+        h_grouped = {}
         h_q = {}
         out_rows = out.rearrange("(n p) j -> p n j", p=P)
 
-        def a_tile(b, t):
+        def tanh_rows(b, t):
             cols = slice(P * t, P * (t + 1))
             acc = bank("acc", [P, S], PACK * b + t)
             table = [
                 (
-                    w1_wp[b][:, a, 2 * P * t : 2 * P * (t + 1)].bitcast(FP4X4),
-                    w1_sp[:, K * a + KP * b + P * t : K * a + KP * b + P * (t + 1)],
+                    w1_dealt[b][:, a, 2 * P * t : 2 * P * (t + 1)].bitcast(FP4X4),
+                    weight_s_dealt[:, K * a + KP * b + P * t : K * a + KP * b + P * (t + 1)],
                     v_w[a],
                     v_s[a],
                 )
@@ -313,26 +309,26 @@ def tile_list_ocean_colour_gradient_kernel(
                 )
             nc.scalar.activation(th[b][:, t, :], acc[:], ACT.Tanh)
 
-        def square_tile(b, j):
+        def square(b, j):
             th2[b, j] = held("th2_%d%d" % (b, j), [P, PACK * P], F32, place_of=th2_place[b][j])
             nc.scalar.activation(*group_views(th2[b, j][:], th[b][:, :, P * j : P * (j + 1)]), ACT.Square)
 
-        def h_product(b, j):
+        def h_tile(b, j):
             neg_e = bank("neg_e", [P, PACK, P], JT * b + j)
             adj_cols = slice(P * (j % 2), P * (j % 2 + 1))
             for t in range(PACK):
                 nc.tensor.matmul_mx(
                     out=neg_e[:, t, :],
-                    lhsT=w3_wp[b][:, P * t : P * (t + 1)].bitcast(FP8X4),
-                    lhsT_scale=w1_sp[4:, KP * b + P * t : KP * b + P * (t + 1)],
+                    lhsT=w3_dealt[b][:, P * t : P * (t + 1)].bitcast(FP8X4),
+                    lhsT_scale=weight_s_dealt[W3_SHIFT:, KP * b + P * t : KP * b + P * (t + 1)],
                     rhs=neg_adj_q[j // 2][0][:, adj_cols].bitcast(FP8X4),
                     rhs_scale=neg_adj_q[j // 2][1][:, adj_cols],
                     start=True,
                     stop=True,
                 )
-            h_g[b, j] = held("h_g%d%d" % (b, j), [P, PACK * P], BF16)
+            h_grouped[b, j] = held("h_g%d%d" % (b, j), [P, PACK * P], BF16)
             nc.vector.scalar_tensor_tensor(
-                h_g[b, j][:].rearrange("p (c t) -> p c t", t=PACK),
+                h_grouped[b, j][:].rearrange("p (c t) -> p c t", t=PACK),
                 th2[b, j][:].rearrange("p (c t) -> p c t", t=PACK),
                 1.0,
                 neg_e[:].rearrange("p t c -> p c t"),
@@ -340,14 +336,11 @@ def tile_list_ocean_colour_gradient_kernel(
                 ALU.mult,
             )
 
-        def h_quantize(b, j):
-            codes = held("h%d%d_c" % (b, j), [P, P], U32)
-            scales = held("h%d%d_s" % (b, j), [P, P], U8)
-            nc.vector.quantize_mx(out=codes[:].bitcast(FP8X4), scales=scales[:], in_=h_g[b, j][:])
-            h_q[b, j] = codes, scales
+        def quantize_h(b, j):
+            h_q[b, j] = quantize("h%d%d" % (b, j), [h_grouped[b, j]])
 
-        def out_rows_of(j, first, count, number, copy_out):
-            res = bank("res", [P, count, P], number)
+        def out_block(j, first, count, bank_number, copy_out):
+            res = bank("res", [P, count, P], bank_number)
             for b in range(PASSES):
                 for n in range(count):
                     cols = slice(P * (first + n), P * (first + n + 1))
@@ -366,16 +359,17 @@ def tile_list_ocean_colour_gradient_kernel(
 
         for b in range(PASSES):
             for t in range(PACK):
-                a_tile(b, t)
+                tanh_rows(b, t)
             for j in range(JT):
-                square_tile(b, j)
-        units = [(b, j) for b in range(PASSES) for j in range(JT - 1)] + [(b, JT - 1) for b in range(PASSES)]
-        for i, unit in enumerate(units):
-            h_product(*unit)
+                square(b, j)
+        last = JT - 1
+        h_order = [(b, j) for b in range(PASSES) for j in range(last)] + [(b, last) for b in range(PASSES)]
+        for i, (b, j) in enumerate(h_order):
+            h_tile(b, j)
             if i > 0:
-                h_quantize(*units[i - 1])
-        h_quantize(*units[-1])
-        for j in range(JT - 1):
-            out_rows_of(j, 0, JT, j, on_scalar)
-        out_rows_of(JT - 1, 0, 2, JT - 1, on_vector)
-        out_rows_of(JT - 1, 2, 2, JT, on_scalar)
+                quantize_h(*h_order[i - 1])
+        quantize_h(*h_order[-1])
+        for j in range(last):
+            out_block(j, 0, JT, j, on_scalar)
+        out_block(last, 0, JT // 2, last, on_vector)
+        out_block(last, JT // 2, JT // 2, JT, on_scalar)

@@ -1,7 +1,6 @@
 from contextlib import ExitStack
 
 import concourse.mybir as mybir
-from concourse.masks import make_identity
 
 K, T, S, M = 1024, 2048, 512, 512
 FLOPS = 2 * S * (2 * K * K + M * K + K * S)
@@ -29,7 +28,6 @@ ROWS = 4
 TAB_SHIFT = 16
 W3_SHIFT = 4
 SCALE_SPAN = 3 * QUAD + ROWS
-X_BANK = 4
 
 
 def tile_list_ocean_colour_gradient_kernel(
@@ -38,7 +36,6 @@ def tile_list_ocean_colour_gradient_kernel(
     nc = tc.nc
     with ExitStack() as ctx:
         keep = ctx.enter_context(tc.tile_pool(name="keep", bufs=1))
-        ring = ctx.enter_context(tc.tile_pool(name="ring", bufs=2))
         psum = ctx.enter_context(tc.psum_pool(name="psum", bufs=1))
 
         def held(name, shape, dtype, place_of=None):
@@ -63,12 +60,10 @@ def tile_list_ocean_colour_gradient_kernel(
         weight_s_dealt = held("weight_s_dealt", [P, PASSES * K], U8)
         w3_dealt = [held("w3_dealt%d" % b, [P, KP], U32) for b in range(PASSES)]
         subtrahend = [[held("subtrahend%d%d" % (t, h), [P, HALF], F32) for h in range(2)] for t in range(PACK)]
-        ident = held("ident", [P, P], F32)
 
         nc.vector.memset(tab_s[:].bitcast(I32), 0)
         nc.vector.memset(weight_s[:].rearrange("p a r -> p (a r)").bitcast(I32), 0)
         nc.vector.memset(v_s[1][:].bitcast(I32), 0)
-        make_identity(nc, ident[:])
 
         x_rows = xT.rearrange("(a p t) c -> a t p c", a=PASSES, t=PACK)
 
@@ -167,45 +162,8 @@ def tile_list_ocean_colour_gradient_kernel(
                 tiles.append(grouped)
             return tiles
 
-        def x_by_transposes(a):
-            turned = []
-            for u in range(2):
-                sums = [bank("x_sum", [P, 2, 2, P], X_BANK + 2 * u + h) for h in range(2)]
-                for odd in range(2):
-                    plane = planes[a][2 * u + odd]
-                    plus = ring.tile([P, S], F32, name="plus")
-                    minus = ring.tile([P, S], F32, name="minus")
-                    picked = ring.tile([P, S], F32, name="picked")
-                    nc.vector.tensor_copy(picked[:], plane[:].indirect(idx3[:]))
-                    nc.scalar.activation(minus[:], picked[:], ACT.Copy, scale=-1.0)
-                    nc.vector.tensor_copy(plus[:], plane[:].indirect(idx2[:]))
-                    for j in range(JT):
-                        cols = slice(P * j, P * (j + 1))
-                        dst = sums[j // 2][:, j % 2, odd, :]
-                        nc.tensor.matmul(dst, minus[:, cols], ident[:], start=True, stop=False, is_transpose=True)
-                        nc.tensor.matmul(dst, plus[:, cols], ident[:], start=False, stop=True, is_transpose=True)
-                for h in range(2):
-                    pairs = ring.tile([P, 2, 2 * P], BF16, name="x_pairs", align_bytes=64)
-                    nc.scalar.copy(
-                        pairs[:].rearrange("p i (m odd) -> p i m odd", odd=2),
-                        sums[h][:].rearrange("p i odd m -> p i m odd"),
-                    )
-                    if u == 0:
-                        turned.append(bank("x_turned", [P, 2, 2, P], X_BANK + h))
-                    for i in range(2):
-                        nc.tensor.transpose(turned[h][:, i, u, :], pairs[:, i, :].bitcast(F32), ident[:])
-            parts = []
-            for h in range(2):
-                grouped = ring.tile([P, PACK * HALF], BF16, name="x_g", align_bytes=64)
-                nc.scalar.copy(
-                    grouped[:].bitcast(F32).rearrange("p (i m u) -> p i m u", i=2, u=2),
-                    turned[h][:].rearrange("p i u m -> p i m u"),
-                )
-                parts.append(grouped)
-            return parts
-
-        def x_by_subtraction(a):
-            diff = [held("diff%d" % h, [P, PACK, HALF], F32, place_of="plane0%d" % (2 + h)) for h in range(2)]
+        def gather_x(a, diff_places):
+            diff = [held("diff%d%d" % (a, h), [P, PACK, HALF], F32, place_of=diff_places[h]) for h in range(2)]
             offsets = [slice(LIST_COLS // 2 * h, LIST_COLS // 2 * (h + 1)) for h in range(2)]
             for t in range(PACK):
                 for h in range(2):
@@ -259,8 +217,8 @@ def tile_list_ocean_colour_gradient_kernel(
 
         on_scalar, on_vector = nc.scalar.copy, nc.vector.tensor_copy
 
-        x0_grouped = x_by_transposes(0)
-        x1_float = x_by_subtraction(1)
+        x0_grouped = round_parts("x0", gather_x(0, [None, None]), on_scalar)
+        x1_float = gather_x(1, ["plane02", "plane03"])
         x_q = [quantize("x0", x0_grouped, "subtrahend10")]
         deal_scales()
         w2_q = {(0, 0): prepare_w2(0, 0, on_scalar, "subtrahend30")}
@@ -339,7 +297,7 @@ def tile_list_ocean_colour_gradient_kernel(
         def quantize_h(b, j):
             h_q[b, j] = quantize("h%d%d" % (b, j), [h_grouped[b, j]])
 
-        def out_block(j, first, count, bank_number, copy_out):
+        def out_block(j, first, count, bank_number, copy_out, queue):
             res = bank("res", [P, count, P], bank_number)
             for b in range(PASSES):
                 for n in range(count):
@@ -355,7 +313,7 @@ def tile_list_ocean_colour_gradient_kernel(
                     )
             staged = held("staged%d%d" % (j, first), [P, count, P], F32)
             copy_out(staged[:], res[:])
-            nc.sync.dma_start(out_rows[:, first : first + count, P * j : P * (j + 1)], staged[:])
+            queue.dma_start(out_rows[:, first : first + count, P * j : P * (j + 1)], staged[:])
 
         for b in range(PASSES):
             for t in range(PACK):
@@ -370,6 +328,6 @@ def tile_list_ocean_colour_gradient_kernel(
                 quantize_h(*h_order[i - 1])
         quantize_h(*h_order[-1])
         for j in range(last):
-            out_block(j, 0, JT, j, on_scalar)
-        out_block(last, 0, JT // 2, last, on_vector)
-        out_block(last, JT // 2, JT // 2, JT, on_scalar)
+            out_block(j, 0, JT, j, on_scalar, nc.sync)
+        out_block(last, 0, JT // 2, last, on_vector, nc.sync)
+        out_block(last, JT // 2, JT // 2, JT, on_scalar, nc.scalar)

@@ -57,7 +57,7 @@ def tile_list_ocean_colour_gradient_kernel(
         w2_raw = [[held("w2_raw%d%d" % (a, b), [P, PACK, KP], F32) for b in range(PASSES)] for a in range(PASSES)]
         adj_raw = [held("adj_raw%d" % h, [P, PACK, HALF], F32) for h in range(2)]
         w1_dealt = [held("w1_dealt%d" % b, [P, PASSES, 2 * KP], U8) for b in range(PASSES)]
-        weight_s_dealt = held("weight_s_dealt", [P, PASSES * K], U8)
+        weight_s_dealt = held("weight_s_dealt", [P, PASSES * K], U8, place_of="diff01")
         w3_dealt = [held("w3_dealt%d" % b, [P, KP], U32) for b in range(PASSES)]
         subtrahend = [[held("subtrahend%d%d" % (t, h), [P, HALF], F32) for h in range(2)] for t in range(PACK)]
 
@@ -96,17 +96,17 @@ def tile_list_ocean_colour_gradient_kernel(
         def load_table_scales():
             rows = tab_scales.rearrange("a (q i) n -> i q a n", i=ROWS).bitcast(I32)
             for i in range(ROWS):
-                nc.sync.dma_start(tab_s[i:P:TAB_SHIFT, :].bitcast(I32), rows[i])
+                nc.gpsimd.dma_start(tab_s[i:P:TAB_SHIFT, :].bitcast(I32), rows[i])
 
         def load_w1_scales():
             rows = w1_scales.rearrange("a (q i) y -> i q a y", i=ROWS).bitcast(I32)
             for i in range(ROWS):
-                nc.sync.dma_start(weight_s[i:P:QUAD].bitcast(I32), rows[i])
+                nc.gpsimd.dma_start(weight_s[i:P:QUAD].bitcast(I32), rows[i])
 
         def load_w3_scales():
             rows = w3_scales[0].rearrange("(q i) y -> i q y", i=ROWS).bitcast(I32)
             for i in range(ROWS):
-                nc.sync.dma_start(weight_s[W3_SHIFT + i : P : QUAD, 0, :].bitcast(I32), rows[i])
+                nc.gpsimd.dma_start(weight_s[W3_SHIFT + i : P : QUAD, 0, :].bitcast(I32), rows[i])
 
         load_plane(0, 0)
         nc.sync.dma_start(idx3[:], offs3)

@@ -25,9 +25,8 @@ HALF = S // 2
 LIST_COLS = S // 16
 QUAD = 32
 ROWS = 4
-TAB_SHIFT = 16
+SCALE_ROWS = KP // 32
 W3_SHIFT = 4
-SCALE_SPAN = 3 * QUAD + ROWS
 
 
 def tile_list_ocean_colour_gradient_kernel(
@@ -50,20 +49,24 @@ def tile_list_ocean_colour_gradient_kernel(
         planes = [[held("plane%d%d" % (a, t), [P, T], F32) for t in range(PACK)] for a in range(PASSES)]
         tab_w = [held("tab_w%d" % a, [P, T], U32) for a in range(PASSES)]
         tab_s = held("tab_s", [P, T], U8)
+        picked_s = held("picked_s", [P, S], U8)
         v_s = [held("v_s%d" % a, [P, S], U8) for a in range(PASSES)]
         w1_w = [held("w1_w%d" % b, [P, PASSES, 2 * KP], U8) for b in range(PASSES)]
-        weight_s = held("weight_s", [P, PASSES, K], U8)
+        weight_s = held("weight_s", [P, K], U8)
+        weight_s_dealt = held("weight_s_dealt", [P, K], U8)
+        w_s = [held("w_s%d" % a, [P, K], U8) for a in range(PASSES)]
         w3_w = [held("w3_w%d" % b, [P, KP], U32) for b in range(PASSES)]
         w2_raw = [[held("w2_raw%d%d" % (a, b), [P, PACK, KP], F32) for b in range(PASSES)] for a in range(PASSES)]
         adj_raw = [held("adj_raw%d" % h, [P, PACK, HALF], F32) for h in range(2)]
         w1_dealt = [held("w1_dealt%d" % b, [P, PASSES, 2 * KP], U8) for b in range(PASSES)]
-        weight_s_dealt = held("weight_s_dealt", [P, PASSES * K], U8, place_of="diff01")
         w3_dealt = [held("w3_dealt%d" % b, [P, KP], U32) for b in range(PASSES)]
         subtrahend = [[held("subtrahend%d%d" % (t, h), [P, HALF], F32) for h in range(2)] for t in range(PACK)]
 
-        nc.vector.memset(tab_s[:].bitcast(I32), 0)
-        nc.vector.memset(weight_s[:].rearrange("p a r -> p (a r)").bitcast(I32), 0)
-        nc.vector.memset(v_s[1][:].bitcast(I32), 0)
+        for tile in (weight_s, tab_s):
+            nc.vector.memset(tile[QUAD : 2 * QUAD, :].bitcast(I32), 0)
+            nc.vector.memset(tile[2 * QUAD :, :].bitcast(I32), 0)
+        for tile in v_s + w_s:
+            nc.vector.memset(tile[:].bitcast(I32), 0)
 
         x_rows = xT.rearrange("(a p t) c -> a t p c", a=PASSES, t=PACK)
 
@@ -93,35 +96,33 @@ def tile_list_ocean_colour_gradient_kernel(
             words = w3_words[0].rearrange("p n t -> p (n t)").bitcast(I32)
             nc.sync.dma_start(w3_w[b][:].bitcast(I32), words[:, KP * b : KP * (b + 1)])
 
-        def load_table_scales():
-            rows = tab_scales.rearrange("a (q i) n -> i q a n", i=ROWS).bitcast(I32)
+        def place_scale_rows(plane, shift, rows, first):
             for i in range(ROWS):
-                nc.gpsimd.dma_start(tab_s[i:P:TAB_SHIFT, :].bitcast(I32), rows[i])
+                nc.gpsimd.dma_start(
+                    plane[shift + i : P : QUAD, :].bitcast(I32),
+                    rows[first + i : first + SCALE_ROWS : ROWS, :].bitcast(I32),
+                )
 
-        def load_w1_scales():
-            rows = w1_scales.rearrange("a (q i) y -> i q a y", i=ROWS).bitcast(I32)
-            for i in range(ROWS):
-                nc.gpsimd.dma_start(weight_s[i:P:QUAD].bitcast(I32), rows[i])
-
-        def load_w3_scales():
-            rows = w3_scales[0].rearrange("(q i) y -> i q y", i=ROWS).bitcast(I32)
-            for i in range(ROWS):
-                nc.gpsimd.dma_start(weight_s[W3_SHIFT + i : P : QUAD, 0, :].bitcast(I32), rows[i])
+        nc.sync.dma_start(tab_s[0:QUAD, :].bitcast(I32), tab_scales.rearrange("a g n -> (a g) n").bitcast(I32))
+        nc.sync.dma_start(idx[:], offs)
+        nc.scalar.dma_start(weight_s[0:QUAD, :].bitcast(I32), w1_scales.rearrange("a g y -> (a g) y").bitcast(I32))
+        nc.scalar.dma_start(weight_s[QUAD : QUAD + SCALE_ROWS, :].bitcast(I32), w3_scales[0].bitcast(I32))
+        nc.vector.tensor_copy(picked_s[:], tab_s[:].indirect(idx[:]))
+        nc.vector.tensor_copy(
+            weight_s_dealt[:].rearrange("p (b t m) -> p b t m", t=PACK, m=P),
+            weight_s[:].rearrange("p (b m t) -> p b t m", t=PACK, m=P),
+        )
+        for a in range(PASSES):
+            place_scale_rows(v_s[a], 0, picked_s, SCALE_ROWS * a)
+            place_scale_rows(w_s[a], 0, weight_s_dealt, SCALE_ROWS * a)
+        place_scale_rows(w_s[0], W3_SHIFT, weight_s_dealt, QUAD)
 
         load_plane(0, 0)
         nc.sync.dma_start(idx3[:], offs3)
         nc.sync.dma_start(idx2[:], offs2)
         load_plane(0, 1)
-        load_table_scales()
         load_plane(0, 2)
-        load_w1_scales()
         load_plane(0, 3)
-        load_w3_scales()
-        nc.sync.dma_start(idx[:], offs)
-        nc.vector.tensor_copy(v_s[0][:], tab_s[:].indirect(idx[:]))
-        nc.scalar.dma_start(
-            v_s[1][0:SCALE_SPAN, :].bitcast(I32), v_s[0][TAB_SHIFT : TAB_SHIFT + SCALE_SPAN, :].bitcast(I32)
-        )
         load_plane(1, 0)
         load_plane(1, 1)
         load_w2(0, 0)
@@ -190,12 +191,6 @@ def tile_list_ocean_colour_gradient_kernel(
             )
             return quantize("w2_%d%d" % (a, b), [grouped], codes_place)
 
-        def deal_scales():
-            nc.vector.tensor_copy(
-                weight_s_dealt[:].rearrange("p (g t m) -> p g t m", t=PACK, m=P),
-                weight_s[:].rearrange("p a r -> p (a r)").rearrange("p (g m t) -> p g t m", t=PACK, m=P),
-            )
-
         def deal_w1(b):
             nc.vector.tensor_copy(
                 w1_dealt[b][:].bitcast(U16).rearrange("p a (t m) -> p a t m", t=PACK),
@@ -220,7 +215,6 @@ def tile_list_ocean_colour_gradient_kernel(
         x0_grouped = round_parts("x0", gather_x(0, [None, None]), on_scalar)
         x1_float = gather_x(1, ["plane02", "plane03"])
         x_q = [quantize("x0", x0_grouped, "subtrahend10")]
-        deal_scales()
         w2_q = {(0, 0): prepare_w2(0, 0, on_scalar, "subtrahend30")}
         w2_q[1, 0] = prepare_w2(1, 0, on_scalar, "subtrahend31")
         deal_w1(0)
@@ -247,7 +241,7 @@ def tile_list_ocean_colour_gradient_kernel(
             table = [
                 (
                     w1_dealt[b][:, a, 2 * P * t : 2 * P * (t + 1)].bitcast(FP4X4),
-                    weight_s_dealt[:, K * a + KP * b + P * t : K * a + KP * b + P * (t + 1)],
+                    w_s[a][:, KP * b + P * t : KP * b + P * (t + 1)],
                     v_w[a],
                     v_s[a],
                 )
@@ -278,7 +272,7 @@ def tile_list_ocean_colour_gradient_kernel(
                 nc.tensor.matmul_mx(
                     out=neg_e[:, t, :],
                     lhsT=w3_dealt[b][:, P * t : P * (t + 1)].bitcast(FP8X4),
-                    lhsT_scale=weight_s_dealt[W3_SHIFT:, KP * b + P * t : KP * b + P * (t + 1)],
+                    lhsT_scale=w_s[0][W3_SHIFT:, KP * b + P * t : KP * b + P * (t + 1)],
                     rhs=neg_adj_q[j // 2][0][:, adj_cols].bitcast(FP8X4),
                     rhs_scale=neg_adj_q[j // 2][1][:, adj_cols],
                     start=True,

@@ -53,7 +53,7 @@ def tile_list_ocean_colour_gradient_kernel(
         v_s = [held("v_s%d" % a, [P, S], U8) for a in range(PASSES)]
         w1_w = [held("w1_w%d" % b, [P, PASSES, 2 * KP], U8) for b in range(PASSES)]
         weight_s = held("weight_s", [P, K], U8)
-        weight_s_dealt = held("weight_s_dealt", [P, K], U8)
+        weight_s_dealt = held("weight_s_dealt", [P, K], U8, place_of="tab_s")
         w_s = [held("w_s%d" % a, [P, K], U8) for a in range(PASSES)]
         w3_w = [held("w3_w%d" % b, [P, KP], U32) for b in range(PASSES)]
         w2_raw = [[held("w2_raw%d%d" % (a, b), [P, PACK, KP], F32) for b in range(PASSES)] for a in range(PASSES)]
@@ -62,9 +62,10 @@ def tile_list_ocean_colour_gradient_kernel(
         w3_dealt = [held("w3_dealt%d" % b, [P, KP], U32) for b in range(PASSES)]
         subtrahend = [[held("subtrahend%d%d" % (t, h), [P, HALF], F32) for h in range(2)] for t in range(PACK)]
 
-        for tile in (weight_s, tab_s):
-            nc.vector.memset(tile[QUAD : 2 * QUAD, :].bitcast(I32), 0)
-            nc.vector.memset(tile[2 * QUAD :, :].bitcast(I32), 0)
+        nc.vector.memset(weight_s[3 * QUAD :, :].bitcast(I32), 0)
+        nc.vector.memset(weight_s[: 2 * QUAD, :].bitcast(I32), 0)
+        nc.vector.memset(tab_s[QUAD : 2 * QUAD, :].bitcast(I32), 0)
+        nc.vector.memset(tab_s[2 * QUAD :, :].bitcast(I32), 0)
         for tile in v_s + w_s:
             nc.vector.memset(tile[:].bitcast(I32), 0)
 
@@ -105,8 +106,8 @@ def tile_list_ocean_colour_gradient_kernel(
 
         nc.sync.dma_start(tab_s[0:QUAD, :].bitcast(I32), tab_scales.rearrange("a g n -> (a g) n").bitcast(I32))
         nc.sync.dma_start(idx[:], offs)
-        nc.scalar.dma_start(weight_s[0:QUAD, :].bitcast(I32), w1_scales.rearrange("a g y -> (a g) y").bitcast(I32))
-        nc.scalar.dma_start(weight_s[QUAD : QUAD + SCALE_ROWS, :].bitcast(I32), w3_scales[0].bitcast(I32))
+        nc.scalar.dma_start(weight_s[2 * QUAD : 3 * QUAD, :].bitcast(I32), w1_scales.rearrange("a g y -> (a g) y").bitcast(I32))
+        nc.scalar.dma_start(weight_s[3 * QUAD : 3 * QUAD + SCALE_ROWS, :].bitcast(I32), w3_scales[0].bitcast(I32))
         nc.vector.tensor_copy(picked_s[:], tab_s[:].indirect(idx[:]))
         nc.vector.tensor_copy(
             weight_s_dealt[:].rearrange("p (b t m) -> p b t m", t=PACK, m=P),
@@ -114,8 +115,8 @@ def tile_list_ocean_colour_gradient_kernel(
         )
         for a in range(PASSES):
             place_scale_rows(v_s[a], 0, picked_s, SCALE_ROWS * a)
-            place_scale_rows(w_s[a], 0, weight_s_dealt, SCALE_ROWS * a)
-        place_scale_rows(w_s[0], W3_SHIFT, weight_s_dealt, QUAD)
+            place_scale_rows(w_s[a], 0, weight_s_dealt, 2 * QUAD + SCALE_ROWS * a)
+        place_scale_rows(w_s[0], W3_SHIFT, weight_s_dealt, 3 * QUAD)
 
         load_plane(0, 0)
         nc.sync.dma_start(idx3[:], offs3)
@@ -132,8 +133,8 @@ def tile_list_ocean_colour_gradient_kernel(
         load_w1(0)
         load_table(0)
         load_table(1)
-        load_w1(1)
         load_w2(0, 1)
+        load_w1(1)
         load_w2(1, 1)
         load_w3(0)
         load_adj(0)

@@ -128,13 +128,13 @@ def tile_list_ocean_colour_gradient_kernel(
         load_plane(1, 1)
         load_w2(0, 0)
         load_plane(1, 2)
-        load_w2(1, 0)
         load_plane(1, 3)
+        load_w2(1, 0)
         load_w1(0)
         load_table(0)
         load_table(1)
-        load_w2(0, 1)
         load_w1(1)
+        load_w2(0, 1)
         load_w2(1, 1)
         load_w3(0)
         load_adj(0)
@@ -184,6 +184,15 @@ def tile_list_ocean_colour_gradient_kernel(
             nc.vector.tensor_copy(words[:], tab_w[a][:].indirect(idx[:]))
             return words
 
+        def prepare_w2_pairs(a, b, round_copy):
+            raw = w2_raw[a][b][:].rearrange("p i (m t) -> p m i t", t=PACK)
+            parts = []
+            for u in range(2):
+                grouped = held("w2_g%d%d%d" % (a, b, u), [P, 2 * KP], BF16)
+                round_copy(grouped[:].rearrange("p (t m i) -> p m i t", t=2, i=PACK), raw[:, :, :, 2 * u : 2 * u + 2])
+                parts.append(grouped)
+            return quantize("w2_%d%d" % (a, b), parts)
+
         def prepare_w2(a, b, round_copy, codes_place=None):
             grouped = held("w2_g%d%d" % (a, b), [P, PACK * KP], BF16)
             round_copy(
@@ -220,17 +229,20 @@ def tile_list_ocean_colour_gradient_kernel(
         w2_q[1, 0] = prepare_w2(1, 0, on_scalar, "subtrahend31")
         deal_w1(0)
         v_w = [gather_table(0)]
-        x_q.append(quantize("x1", round_parts("x1", x1_float, on_scalar)))
+        x1_grouped = held("x1_g", [P, 2, PACK * HALF], BF16, place_of="w2_raw10")
+        for h in range(2):
+            on_scalar(*group_views(x1_grouped[:, h, :], x1_float[h]))
+        x_q.append(quantize("x1", [x1_grouped[:, h, :] for h in range(2)]))
         v_w.append(gather_table(1))
         deal_w1(1)
-        w2_q[0, 1] = prepare_w2(0, 1, on_vector)
+        w2_q[0, 1] = prepare_w2_pairs(0, 1, on_vector)
         w2_q[1, 1] = prepare_w2(1, 1, on_vector)
         deal_w3(0)
         neg_adj_q = [prepare_neg_adj(h) for h in range(2)]
         deal_w3(1)
 
         th = [held("th%d" % b, [P, PACK, S], F32, place_of="plane0%d" % b) for b in range(PASSES)]
-        th2_place = [["plane02", "plane03", "plane10", "tab_s"], ["w2_raw00", "w2_raw10", "tab_w1", "w2_raw01"]]
+        th2_place = [["plane02", "plane03", "plane10", "tab_s"], ["w2_raw00", "plane11", "tab_w1", "w2_raw01"]]
         th2 = {}
         h_grouped = {}
         h_q = {}
@@ -261,6 +273,36 @@ def tile_list_ocean_colour_gradient_kernel(
                     stop=(i == len(passes) - 1),
                 )
             nc.scalar.activation(th[b][:, t, :], acc[:], ACT.Tanh)
+
+        def tanh_entries(b, j):
+            entries = slice(P * j, P * (j + 1))
+            acc = bank("acc", [P, PACK, P], PACK * b + j)
+            passes = []
+            for a in range(PASSES):
+                for t in range(PACK):
+                    lhsT = w1_dealt[b][:, a, 2 * P * t : 2 * P * (t + 1)].bitcast(FP4X4)
+                    passes.append((t, lhsT, w_s[a][:, KP * b + P * t : KP * b + P * (t + 1)], v_w[a], v_s[a]))
+            for a in range(PASSES):
+                for t in range(PACK):
+                    cols = slice(P * t, P * (t + 1))
+                    passes.append((t, w2_q[a, b][0][:, cols].bitcast(FP8X4), w2_q[a, b][1][:, cols], *x_q[a]))
+            for i, (t, lhsT, lhsT_scale, words, scales) in enumerate(passes):
+                nc.tensor.matmul_mx(
+                    out=acc[:, t, :],
+                    lhsT=lhsT,
+                    lhsT_scale=lhsT_scale,
+                    rhs=words[:, entries].bitcast(FP8X4),
+                    rhs_scale=scales[:, entries],
+                    start=(i == 0),
+                    stop=(i == len(passes) - 1),
+                )
+            nc.scalar.activation(
+                th[b][:, j, :].rearrange("p (c t) -> p c t", t=PACK), acc[:].rearrange("p t c -> p c t"), ACT.Tanh
+            )
+
+        def square_entries(b, j):
+            th2[b, j] = held("th2_%d%d" % (b, j), [P, PACK * P], F32, place_of=th2_place[b][j])
+            nc.scalar.activation(th2[b, j][:], th[b][:, j, :], ACT.Square)
 
         def square(b, j):
             th2[b, j] = held("th2_%d%d" % (b, j), [P, PACK * P], F32, place_of=th2_place[b][j])
@@ -310,11 +352,15 @@ def tile_list_ocean_colour_gradient_kernel(
             copy_out(staged[:], res[:])
             queue.dma_start(out_rows[:, first : first + count, P * j : P * (j + 1)], staged[:])
 
-        for b in range(PASSES):
-            for t in range(PACK):
-                tanh_rows(b, t)
-            for j in range(JT):
-                square(b, j)
+        for t in range(PACK):
+            tanh_rows(0, t)
+        for j in range(JT):
+            square(0, j)
+        for j in range(JT):
+            tanh_entries(1, j)
+            if j > 0:
+                square_entries(1, j - 1)
+        square_entries(1, JT - 1)
         last = JT - 1
         h_order = [(b, j) for b in range(PASSES) for j in range(last)] + [(b, last) for b in range(PASSES)]
         for i, (b, j) in enumerate(h_order):

@@ -38,7 +38,7 @@ def tile_list_ocean_colour_gradient_kernel(
         psum = ctx.enter_context(tc.psum_pool(name="psum", bufs=1))
 
         def held(name, shape, dtype, place_of=None):
-            return keep.tile(shape, dtype, name=name, tag=place_of or name, align_bytes=64)
+            return keep.tile(shape, dtype, name=name, tag=place_of or name, align_bytes=256)
 
         def bank(name, shape, number):
             return psum.tile(shape, F32, name=name, tag="bank%d" % number)
@@ -243,6 +243,7 @@ def tile_list_ocean_colour_gradient_kernel(
 
         th = [held("th%d" % b, [P, PACK, S], F32, place_of="plane0%d" % b) for b in range(PASSES)]
         th2_place = [["plane02", "plane03", "plane10", "tab_s"], ["w2_raw00", "plane11", "tab_w1", "w2_raw01"]]
+        staged_place = {(0, 0): "plane12", (1, 0): "plane13", (2, 0): "w2_raw11"}
         th2 = {}
         h_grouped = {}
         h_q = {}
@@ -348,7 +349,7 @@ def tile_list_ocean_colour_gradient_kernel(
                         start=(b == 0 and n == 0),
                         stop=(b == PASSES - 1 and n == count - 1),
                     )
-            staged = held("staged%d%d" % (j, first), [P, count, P], F32)
+            staged = held("staged%d%d" % (j, first), [P, count, P], F32, place_of=staged_place.get((j, first)))
             copy_out(staged[:], res[:])
             queue.dma_start(out_rows[:, first : first + count, P * j : P * (j + 1)], staged[:])
 

@@ -232,7 +232,7 @@ def tile_list_ocean_colour_gradient_kernel(
         x1_grouped = held("x1_g", [P, 2, PACK * HALF], BF16, place_of="w2_raw10")
         for h in range(2):
             on_scalar(*group_views(x1_grouped[:, h, :], x1_float[h]))
-        x_q.append(quantize("x1", [x1_grouped[:, h, :] for h in range(2)]))
+        x_q.append(quantize("x1", [x1_grouped[:, h, :] for h in range(2)], "tab_w0"))
         v_w.append(gather_table(1))
         deal_w1(1)
         w2_q[0, 1] = prepare_w2_pairs(0, 1, on_vector)

@@ -56,7 +56,8 @@ def tile_list_ocean_colour_gradient_kernel(
         weight_s_dealt = held("weight_s_dealt", [P, K], U8, place_of="tab_s")
         w_s = [held("w_s%d" % a, [P, K], U8) for a in range(PASSES)]
         w3_w = [held("w3_w%d" % b, [P, KP], U32) for b in range(PASSES)]
-        w2_raw = [[held("w2_raw%d%d" % (a, b), [P, PACK, KP], F32) for b in range(PASSES)] for a in range(PASSES)]
+        w2_raw = [held("w2_raw%d0" % a, [P, PACK, KP], F32) for a in range(PASSES)]
+        w2_late = [[held("w2_late%d%d" % (a, u), [P, PACK, KP // 2], F32) for u in range(2)] for a in range(PASSES)]
         adj_raw = [held("adj_raw%d" % h, [P, PACK, HALF], F32) for h in range(2)]
         w1_dealt = [held("w1_dealt%d" % b, [P, PASSES, 2 * KP], U8) for b in range(PASSES)]
         w3_dealt = [held("w3_dealt%d" % b, [P, KP], U32) for b in range(PASSES)]
@@ -77,11 +78,15 @@ def tile_list_ocean_colour_gradient_kernel(
         def load_table(a):
             nc.sync.dma_start(tab_w[a][:].bitcast(I32), tab_words[a].rearrange("p n t -> p (n t)").bitcast(I32))
 
-        def load_w2(a, b):
-            nc.sync.dma_start(
-                w2_raw[a][b][:],
-                w2[KP * a : KP * (a + 1), KP * b : KP * (b + 1)].rearrange("(p t) c -> p t c", t=PACK),
-            )
+        def w2_rows(a, b):
+            return w2[KP * a : KP * (a + 1), KP * b : KP * (b + 1)].rearrange("(p t) c -> p t c", t=PACK)
+
+        def load_w2(a):
+            nc.sync.dma_start(w2_raw[a][:], w2_rows(a, 0))
+
+        def load_w2_late(a):
+            for u in range(2):
+                nc.sync.dma_start(w2_late[a][u][:], w2_rows(a, 1)[:, :, KP // 2 * u : KP // 2 * (u + 1)])
 
         def load_w1(b):
             nc.sync.dma_start(
@@ -126,16 +131,16 @@ def tile_list_ocean_colour_gradient_kernel(
         load_plane(0, 3)
         load_plane(1, 0)
         load_plane(1, 1)
-        load_w2(0, 0)
+        load_w2(0)
         load_plane(1, 2)
         load_plane(1, 3)
-        load_w2(1, 0)
+        load_w2(1)
         load_w1(0)
         load_table(0)
         load_table(1)
         load_w1(1)
-        load_w2(0, 1)
-        load_w2(1, 1)
+        load_w2_late(0)
+        load_w2_late(1)
         load_w3(0)
         load_adj(0)
         load_adj(1)
@@ -184,20 +189,20 @@ def tile_list_ocean_colour_gradient_kernel(
             nc.vector.tensor_copy(words[:], tab_w[a][:].indirect(idx[:]))
             return words
 
-        def prepare_w2_pairs(a, b, round_copy):
-            raw = w2_raw[a][b][:].rearrange("p i (m t) -> p m i t", t=PACK)
-            parts = []
+        def prepare_w2_late(a):
+            grouped = held("w2_g%d1" % a, [P, PACK * KP], BF16)
+            places = grouped[:].rearrange("p (t m i) -> p m i t", t=PACK, i=PACK)
             for u in range(2):
-                grouped = held("w2_g%d%d%d" % (a, b, u), [P, 2 * KP], BF16)
-                round_copy(grouped[:].rearrange("p (t m i) -> p m i t", t=2, i=PACK), raw[:, :, :, 2 * u : 2 * u + 2])
-                parts.append(grouped)
-            return quantize("w2_%d%d" % (a, b), parts)
+                nc.vector.tensor_copy(
+                    places[:, P // 2 * u : P // 2 * (u + 1), :, :], w2_late[a][u][:].rearrange("p i (m t) -> p m i t", t=PACK)
+                )
+            return quantize("w2_%d1" % a, [grouped])
 
         def prepare_w2(a, b, round_copy, codes_place=None):
             grouped = held("w2_g%d%d" % (a, b), [P, PACK * KP], BF16)
             round_copy(
                 grouped[:].rearrange("p (t m i) -> p m i t", t=PACK, i=PACK),
-                w2_raw[a][b][:].rearrange("p i (m t) -> p m i t", t=PACK),
+                w2_raw[a][:].rearrange("p i (m t) -> p m i t", t=PACK),
             )
             return quantize("w2_%d%d" % (a, b), [grouped], codes_place)
 
@@ -235,15 +240,15 @@ def tile_list_ocean_colour_gradient_kernel(
         x_q.append(quantize("x1", [x1_grouped[:, h, :] for h in range(2)], "tab_w0"))
         v_w.append(gather_table(1))
         deal_w1(1)
-        w2_q[0, 1] = prepare_w2_pairs(0, 1, on_vector)
-        w2_q[1, 1] = prepare_w2(1, 1, on_vector)
+        w2_q[0, 1] = prepare_w2_late(0)
+        w2_q[1, 1] = prepare_w2_late(1)
         deal_w3(0)
         neg_adj_q = [prepare_neg_adj(h) for h in range(2)]
         deal_w3(1)
 
         th = [held("th%d" % b, [P, PACK, S], F32, place_of="plane0%d" % b) for b in range(PASSES)]
-        th2_place = [["plane02", "plane03", "plane10", "tab_s"], ["w2_raw00", "plane11", "tab_w1", "w2_raw01"]]
-        staged_place = {(0, 0): "plane12", (1, 0): "plane13", (2, 0): "w2_raw11"}
+        th2_place = [["plane02", "plane03", "plane10", "tab_s"], ["w2_raw00", "plane11", "tab_w1", "w2_late00"]]
+        staged_place = {(0, 0): "plane12", (1, 0): "plane13", (2, 0): "w2_late10"}
         th2 = {}
         h_grouped = {}
         h_q = {}

@@ -191,25 +191,26 @@ def tile_list_ocean_colour_gradient_kernel(
 
         def prepare_w2_late(a):
             grouped = held("w2_g%d1" % a, [P, PACK * KP], BF16)
-            places = grouped[:].rearrange("p (t m i) -> p m i t", t=PACK, i=PACK)
+            places = grouped[:].rearrange("p (s t m i) -> p s m i t", s=2, t=2, i=PACK)
             for u in range(2):
                 nc.vector.tensor_copy(
-                    places[:, P // 2 * u : P // 2 * (u + 1), :, :], w2_late[a][u][:].rearrange("p i (m t) -> p m i t", t=PACK)
+                    places[:, :, P // 2 * u : P // 2 * (u + 1), :, :],
+                    w2_late[a][u][:].rearrange("p i (m s t) -> p s m i t", s=2, t=2),
                 )
             return quantize("w2_%d1" % a, [grouped])
 
         def prepare_w2(a, b, round_copy, codes_place=None):
             grouped = held("w2_g%d%d" % (a, b), [P, PACK * KP], BF16)
             round_copy(
-                grouped[:].rearrange("p (t m i) -> p m i t", t=PACK, i=PACK),
-                w2_raw[a][:].rearrange("p i (m t) -> p m i t", t=PACK),
+                grouped[:].rearrange("p (s t m i) -> p s m i t", s=2, t=2, i=PACK),
+                w2_raw[a][:].rearrange("p i (m s t) -> p s m i t", s=2, t=2),
             )
             return quantize("w2_%d%d" % (a, b), [grouped], codes_place)
 
         def deal_w1(b):
             nc.vector.tensor_copy(
-                w1_dealt[b][:].bitcast(U16).rearrange("p a (t m) -> p a t m", t=PACK),
-                w1_w[b][:].bitcast(U16).rearrange("p a (m t) -> p a t m", t=PACK),
+                w1_dealt[b][:].bitcast(U16).rearrange("p a (t g i) -> p a g t i", t=PACK, i=8),
+                w1_w[b][:].bitcast(U16).rearrange("p a (g i t) -> p a g t i", t=PACK, i=8),
             )
 
         def deal_w3(b):

from contextlib import ExitStack

import concourse.mybir as mybir

K, T, S, M = 1024, 2048, 512, 512
FLOPS = 2 * S * (2 * K * K + M * K + K * S)

F32 = mybir.dt.float32
BF16 = mybir.dt.bfloat16
I32 = mybir.dt.int32
U32 = mybir.dt.uint32
U16 = mybir.dt.uint16
U8 = mybir.dt.uint8
FP8X4 = mybir.dt.float8_e4m3fn_x4
FP4X4 = mybir.dt.float4_e2m1fn_x4
ACT = mybir.ActivationFunctionType
ALU = mybir.AluOpType

P = 128
PACK = 4
KP = P * PACK
PASSES = K // KP
JT = S // P
HALF = S // 2
LIST_COLS = S // 16
QUAD = 32
ROWS = 4
SCALE_ROWS = KP // 32
W3_SHIFT = 4


def tile_list_ocean_colour_gradient_kernel(
    tc, tab_words, tab_scales, offs, xT, offs2, offs3, w1_words, w1_scales, w2, w3_words, w3_scales, adj, out
):
    nc = tc.nc
    with ExitStack() as ctx:
        keep = ctx.enter_context(tc.tile_pool(name="keep", bufs=1))
        psum = ctx.enter_context(tc.psum_pool(name="psum", bufs=1))

        def held(name, shape, dtype, place_of=None):
            return keep.tile(shape, dtype, name=name, tag=place_of or name, align_bytes=256)

        def bank(name, shape, number):
            return psum.tile(shape, F32, name=name, tag="bank%d" % number)

        idx = keep.tile([P, LIST_COLS], U16, name="idx")
        idx2 = keep.tile([P, LIST_COLS], U16, name="idx2")
        idx3 = keep.tile([P, LIST_COLS], U16, name="idx3")
        planes = [[held("plane%d%d" % (a, t), [P, T], F32) for t in range(PACK)] for a in range(PASSES)]
        tab_w = [held("tab_w%d" % a, [P, T], U32) for a in range(PASSES)]
        tab_s = held("tab_s", [P, T], U8)
        picked_s = held("picked_s", [P, S], U8)
        v_s = [held("v_s%d" % a, [P, S], U8) for a in range(PASSES)]
        w1_w = [held("w1_w%d" % b, [P, PASSES, 2 * KP], U8) for b in range(PASSES)]
        weight_s = held("weight_s", [P, K], U8)
        weight_s_dealt = held("weight_s_dealt", [P, K], U8, place_of="tab_s")
        w_s = [held("w_s%d" % a, [P, K], U8) for a in range(PASSES)]
        w3_w = [held("w3_w%d" % b, [P, KP], U32) for b in range(PASSES)]
        w2_raw = [held("w2_raw%d0" % a, [P, PACK, KP], F32) for a in range(PASSES)]
        w2_late = [[held("w2_late%d%d" % (a, u), [P, PACK, KP // 2], F32) for u in range(2)] for a in range(PASSES)]
        adj_raw = [held("adj_raw%d" % h, [P, PACK, HALF], F32) for h in range(2)]
        w1_dealt = [held("w1_dealt%d" % b, [P, PASSES, 2 * KP], U8) for b in range(PASSES)]
        w3_dealt = [held("w3_dealt%d" % b, [P, KP], U32) for b in range(PASSES)]
        subtrahend = [[held("subtrahend%d%d" % (t, h), [P, HALF], F32) for h in range(2)] for t in range(PACK)]

        nc.vector.memset(weight_s[3 * QUAD :, :].bitcast(I32), 0)
        nc.vector.memset(weight_s[: 2 * QUAD, :].bitcast(I32), 0)
        nc.vector.memset(tab_s[QUAD : 2 * QUAD, :].bitcast(I32), 0)
        nc.vector.memset(tab_s[2 * QUAD :, :].bitcast(I32), 0)
        for tile in v_s + w_s:
            nc.vector.memset(tile[:].bitcast(I32), 0)

        x_rows = xT.rearrange("(a p t) c -> a t p c", a=PASSES, t=PACK)

        def load_plane(a, t):
            nc.sync.dma_start(planes[a][t][:], x_rows[a, t])

        def load_table(a):
            nc.sync.dma_start(tab_w[a][:].bitcast(I32), tab_words[a].rearrange("p n t -> p (n t)").bitcast(I32))

        def w2_rows(a, b):
            return w2[KP * a : KP * (a + 1), KP * b : KP * (b + 1)].rearrange("(p t) c -> p t c", t=PACK)

        def load_w2(a):
            nc.sync.dma_start(w2_raw[a][:], w2_rows(a, 0))

        def load_w2_late(a):
            for u in range(2):
                nc.sync.dma_start(w2_late[a][u][:], w2_rows(a, 1)[:, :, KP // 2 * u : KP // 2 * (u + 1)])

        def load_w1(b):
            nc.sync.dma_start(
                w1_w[b][:].bitcast(I32),
                w1_words[:, :, 2 * KP * b : 2 * KP * (b + 1)].rearrange("a p y -> p a y").bitcast(I32),
            )

        def load_adj(h):
            rows = adj.rearrange("(p t) c -> p t c", t=PACK)
            nc.sync.dma_start(adj_raw[h][:], rows[:, :, HALF * h : HALF * (h + 1)])

        def load_w3(b):
            words = w3_words[0].rearrange("p n t -> p (n t)").bitcast(I32)
            nc.sync.dma_start(w3_w[b][:].bitcast(I32), words[:, KP * b : KP * (b + 1)])

        def place_scale_rows(plane, shift, rows, first):
            for i in range(ROWS):
                nc.gpsimd.dma_start(
                    plane[shift + i : P : QUAD, :].bitcast(I32),
                    rows[first + i : first + SCALE_ROWS : ROWS, :].bitcast(I32),
                )

        nc.sync.dma_start(tab_s[0:QUAD, :].bitcast(I32), tab_scales.rearrange("a g n -> (a g) n").bitcast(I32))
        nc.sync.dma_start(idx[:], offs)
        nc.scalar.dma_start(weight_s[2 * QUAD : 3 * QUAD, :].bitcast(I32), w1_scales.rearrange("a g y -> (a g) y").bitcast(I32))
        nc.scalar.dma_start(weight_s[3 * QUAD : 3 * QUAD + SCALE_ROWS, :].bitcast(I32), w3_scales[0].bitcast(I32))
        nc.vector.tensor_copy(picked_s[:], tab_s[:].indirect(idx[:]))
        nc.vector.tensor_copy(
            weight_s_dealt[:].rearrange("p (b t m) -> p b t m", t=PACK, m=P),
            weight_s[:].rearrange("p (b m t) -> p b t m", t=PACK, m=P),
        )
        for a in range(PASSES):
            place_scale_rows(v_s[a], 0, picked_s, SCALE_ROWS * a)
            place_scale_rows(w_s[a], 0, weight_s_dealt, 2 * QUAD + SCALE_ROWS * a)
        place_scale_rows(w_s[0], W3_SHIFT, weight_s_dealt, 3 * QUAD)

        load_plane(0, 0)
        nc.sync.dma_start(idx3[:], offs3)
        nc.sync.dma_start(idx2[:], offs2)
        load_plane(0, 1)
        load_plane(0, 2)
        load_plane(0, 3)
        load_plane(1, 0)
        load_plane(1, 1)
        load_w2(0)
        load_plane(1, 2)
        load_plane(1, 3)
        load_w2(1)
        load_w1(0)
        load_table(0)
        load_table(1)
        load_w1(1)
        load_w2_late(0)
        load_w2_late(1)
        load_w3(0)
        load_adj(0)
        load_adj(1)
        load_w3(1)

        def group_views(grouped, raw):
            return (
                grouped.rearrange("p (c i t) -> p c t i", i=4, t=PACK),
                raw.rearrange("p t (c i) -> p c t i", i=4),
            )

        def quantize(name, parts, codes_place=None):
            width = parts[0][:].shape[1] // PACK
            codes = held(name + "_c", [P, width * len(parts)], U32, place_of=codes_place)
            scales = held(name + "_s", [P, width * len(parts)], U8)
            for i, grouped in enumerate(parts):
                cols = slice(width * i, width * (i + 1))
                nc.vector.quantize_mx(out=codes[:, cols].bitcast(FP8X4), scales=scales[:, cols], in_=grouped[:])
            return codes, scales

        def round_parts(name, parts, round_copy):
            tiles = []
            for i, raw in enumerate(parts):
                grouped = held("%s_g%d" % (name, i), [P, PACK * raw.shape[2]], BF16)
                round_copy(*group_views(grouped[:], raw))
                tiles.append(grouped)
            return tiles

        def gather_x(a, diff_places):
            diff = [held("diff%d%d" % (a, h), [P, PACK, HALF], F32, place_of=diff_places[h]) for h in range(2)]
            offsets = [slice(LIST_COLS // 2 * h, LIST_COLS // 2 * (h + 1)) for h in range(2)]
            for t in range(PACK):
                for h in range(2):
                    nc.vector.tensor_copy(subtrahend[t][h][:], planes[a][t][:].indirect(idx3[:, offsets[h]]))
                for h in range(2):
                    nc.vector.tensor_tensor(
                        diff[h][:, t, :],
                        planes[a][t][:].indirect(idx2[:, offsets[h]]),
                        subtrahend[t][h][:],
                        ALU.subtract,
                    )
            return [diff[h][:] for h in range(2)]

        def gather_table(a):
            words = held("v_w%d" % a, [P, S], U32)
            nc.vector.tensor_copy(words[:], tab_w[a][:].indirect(idx[:]))
            return words

        def prepare_w2_late(a):
            grouped = held("w2_g%d1" % a, [P, PACK * KP], BF16)
            places = grouped[:].rearrange("p (s t m i) -> p s m i t", s=2, t=2, i=PACK)
            for u in range(2):
                nc.vector.tensor_copy(
                    places[:, :, P // 2 * u : P // 2 * (u + 1), :, :],
                    w2_late[a][u][:].rearrange("p i (m s t) -> p s m i t", s=2, t=2),
                )
            return quantize("w2_%d1" % a, [grouped])

        def prepare_w2(a, b, round_copy, codes_place=None):
            grouped = held("w2_g%d%d" % (a, b), [P, PACK * KP], BF16)
            round_copy(
                grouped[:].rearrange("p (s t m i) -> p s m i t", s=2, t=2, i=PACK),
                w2_raw[a][:].rearrange("p i (m s t) -> p s m i t", s=2, t=2),
            )
            return quantize("w2_%d%d" % (a, b), [grouped], codes_place)

        def deal_w1(b):
            nc.vector.tensor_copy(
                w1_dealt[b][:].bitcast(U16).rearrange("p a (t g i) -> p a g t i", t=PACK, i=8),
                w1_w[b][:].bitcast(U16).rearrange("p a (g i t) -> p a g t i", t=PACK, i=8),
            )

        def deal_w3(b):
            nc.vector.tensor_copy(
                w3_dealt[b][:].bitcast(I32).rearrange("p (t g i) -> p g t i", t=PACK, i=4),
                w3_w[b][:].bitcast(I32).rearrange("p (g i t) -> p g t i", t=PACK, i=4),
            )

        def negate_on_vector(dst, src):
            nc.vector.tensor_scalar(dst, src, -1.0, None, ALU.mult)

        def prepare_neg_adj(h):
            parts = [adj_raw[h][:, :, P * i : P * (i + 1)] for i in range(2)]
            return quantize("adj%d" % h, round_parts("adj%d" % h, parts, negate_on_vector))

        on_scalar, on_vector = nc.scalar.copy, nc.vector.tensor_copy

        x0_grouped = round_parts("x0", gather_x(0, [None, None]), on_scalar)
        x1_float = gather_x(1, ["plane02", "plane03"])
        x_q = [quantize("x0", x0_grouped, "subtrahend10")]
        w2_q = {(0, 0): prepare_w2(0, 0, on_scalar, "subtrahend30")}
        w2_q[1, 0] = prepare_w2(1, 0, on_scalar, "subtrahend31")
        deal_w1(0)
        v_w = [gather_table(0)]
        x1_grouped = held("x1_g", [P, 2, PACK * HALF], BF16, place_of="w2_raw10")
        for h in range(2):
            on_scalar(*group_views(x1_grouped[:, h, :], x1_float[h]))
        x_q.append(quantize("x1", [x1_grouped[:, h, :] for h in range(2)], "tab_w0"))
        v_w.append(gather_table(1))
        deal_w1(1)
        w2_q[0, 1] = prepare_w2_late(0)
        w2_q[1, 1] = prepare_w2_late(1)
        deal_w3(0)
        neg_adj_q = [prepare_neg_adj(h) for h in range(2)]
        deal_w3(1)

        th = [held("th%d" % b, [P, PACK, S], F32, place_of="plane0%d" % b) for b in range(PASSES)]
        th2_place = [["plane02", "plane03", "plane10", "tab_s"], ["w2_raw00", "plane11", "tab_w1", "w2_late00"]]
        staged_place = {(0, 0): "plane12", (1, 0): "plane13", (2, 0): "w2_late10"}
        th2 = {}
        h_grouped = {}
        h_q = {}
        out_rows = out.rearrange("(n p) j -> p n j", p=P)

        def tanh_rows(b, t):
            cols = slice(P * t, P * (t + 1))
            acc = bank("acc", [P, S], PACK * b + t)
            table = [
                (
                    w1_dealt[b][:, a, 2 * P * t : 2 * P * (t + 1)].bitcast(FP4X4),
                    w_s[a][:, KP * b + P * t : KP * b + P * (t + 1)],
                    v_w[a],
                    v_s[a],
                )
                for a in range(PASSES)
            ]
            bands = [(w2_q[a, b][0][:, cols].bitcast(FP8X4), w2_q[a, b][1][:, cols], *x_q[a]) for a in range(PASSES)]
            passes = [bands[0], table[0], bands[1], table[1]] if b == 0 else table + bands
            for i, (lhsT, lhsT_scale, words, scales) in enumerate(passes):
                nc.tensor.matmul_mx(
                    out=acc[:],
                    lhsT=lhsT,
                    lhsT_scale=lhsT_scale,
                    rhs=words[:].bitcast(FP8X4),
                    rhs_scale=scales[:],
                    start=(i == 0),
                    stop=(i == len(passes) - 1),
                )
            nc.scalar.activation(th[b][:, t, :], acc[:], ACT.Tanh)

        def tanh_entries(b, j):
            entries = slice(P * j, P * (j + 1))
            acc = bank("acc", [P, PACK, P], PACK * b + j)
            passes = []
            for a in range(PASSES):
                for t in range(PACK):
                    lhsT = w1_dealt[b][:, a, 2 * P * t : 2 * P * (t + 1)].bitcast(FP4X4)
                    passes.append((t, lhsT, w_s[a][:, KP * b + P * t : KP * b + P * (t + 1)], v_w[a], v_s[a]))
            for a in range(PASSES):
                for t in range(PACK):
                    cols = slice(P * t, P * (t + 1))
                    passes.append((t, w2_q[a, b][0][:, cols].bitcast(FP8X4), w2_q[a, b][1][:, cols], *x_q[a]))
            for i, (t, lhsT, lhsT_scale, words, scales) in enumerate(passes):
                nc.tensor.matmul_mx(
                    out=acc[:, t, :],
                    lhsT=lhsT,
                    lhsT_scale=lhsT_scale,
                    rhs=words[:, entries].bitcast(FP8X4),
                    rhs_scale=scales[:, entries],
                    start=(i == 0),
                    stop=(i == len(passes) - 1),
                )
            nc.scalar.activation(
                th[b][:, j, :].rearrange("p (c t) -> p c t", t=PACK), acc[:].rearrange("p t c -> p c t"), ACT.Tanh
            )

        def square_entries(b, j):
            th2[b, j] = held("th2_%d%d" % (b, j), [P, PACK * P], F32, place_of=th2_place[b][j])
            nc.scalar.activation(th2[b, j][:], th[b][:, j, :], ACT.Square)

        def square(b, j):
            th2[b, j] = held("th2_%d%d" % (b, j), [P, PACK * P], F32, place_of=th2_place[b][j])
            nc.scalar.activation(*group_views(th2[b, j][:], th[b][:, :, P * j : P * (j + 1)]), ACT.Square)

        def h_tile(b, j):
            neg_e = bank("neg_e", [P, PACK, P], JT * b + j)
            adj_cols = slice(P * (j % 2), P * (j % 2 + 1))
            for t in range(PACK):
                nc.tensor.matmul_mx(
                    out=neg_e[:, t, :],
                    lhsT=w3_dealt[b][:, P * t : P * (t + 1)].bitcast(FP8X4),
                    lhsT_scale=w_s[0][W3_SHIFT:, KP * b + P * t : KP * b + P * (t + 1)],
                    rhs=neg_adj_q[j // 2][0][:, adj_cols].bitcast(FP8X4),
                    rhs_scale=neg_adj_q[j // 2][1][:, adj_cols],
                    start=True,
                    stop=True,
                )
            h_grouped[b, j] = held("h_g%d%d" % (b, j), [P, PACK * P], BF16)
            nc.vector.scalar_tensor_tensor(
                h_grouped[b, j][:].rearrange("p (c t) -> p c t", t=PACK),
                th2[b, j][:].rearrange("p (c t) -> p c t", t=PACK),
                1.0,
                neg_e[:].rearrange("p t c -> p c t"),
                ALU.subtract,
                ALU.mult,
            )

        def quantize_h(b, j):
            h_q[b, j] = quantize("h%d%d" % (b, j), [h_grouped[b, j]])

        def out_block(j, first, count, bank_number, copy_out, queue):
            res = bank("res", [P, count, P], bank_number)
            for b in range(PASSES):
                for n in range(count):
                    cols = slice(P * (first + n), P * (first + n + 1))
                    nc.tensor.matmul_mx(
                        out=res[:, n, :],
                        lhsT=v_w[b][:, cols].bitcast(FP8X4),
                        lhsT_scale=v_s[b][:, cols],
                        rhs=h_q[b, j][0][:].bitcast(FP8X4),
                        rhs_scale=h_q[b, j][1][:],
                        start=(b == 0 and n == 0),
                        stop=(b == PASSES - 1 and n == count - 1),
                    )
            staged = held("staged%d%d" % (j, first), [P, count, P], F32, place_of=staged_place.get((j, first)))
            copy_out(staged[:], res[:])
            queue.dma_start(out_rows[:, first : first + count, P * j : P * (j + 1)], staged[:])

        for t in range(PACK):
            tanh_rows(0, t)
        for j in range(JT):
            square(0, j)
        for j in range(JT):
            tanh_entries(1, j)
            if j > 0:
                square_entries(1, j - 1)
        square_entries(1, JT - 1)
        last = JT - 1
        h_order = [(b, j) for b in range(PASSES) for j in range(last)] + [(b, last) for b in range(PASSES)]
        for i, (b, j) in enumerate(h_order):
            h_tile(b, j)
            if i > 0:
                quantize_h(*h_order[i - 1])
        quantize_h(*h_order[-1])
        for j in range(last):
            out_block(j, 0, JT, j, on_scalar, nc.sync)
        out_block(last, 0, JT // 2, last, on_vector, nc.sync)
        out_block(last, JT // 2, JT // 2, JT, on_scalar, nc.scalar)
